import numpy as np, ml_dtypes
CORES = [48,51,52,55]
N = 4
import mx_ref
BF = ml_dtypes.bfloat16
def gcols(t, e):
    v = np.concatenate([t.reshape(8, 16, -1, 4), np.zeros((8, 16, 1, 4), BF)], axis=2)
    return np.ascontiguousarray(np.stack([v[g][:, e[g]] for g in range(8)])).reshape(128, -1)
def gpick(z, e):
    return np.concatenate([z[16 * g:16 * g + 16][:, e[g]] for g in range(8)])
def tile(rs):
    return np.stack(rs, axis=2).reshape(128, -1).astype(BF)
def pick(q, e):
    c = np.concatenate([q[0].reshape(128, -1, 4), np.zeros((128, 1, 4), np.uint8)], axis=1); s = np.concatenate([q[1], np.ones((16, 1), np.uint8)], axis=1)
    return (np.ascontiguousarray(c[:, e].reshape(128, -1)), np.ascontiguousarray(s[:, e]))
def join(*qs):
    return (np.concatenate([q[0] for q in qs], axis=1), np.concatenate([q[1] for q in qs], axis=1))
def put(q, e, v):
    c, s = q[0].reshape(128, -1, 4).copy(), q[1].copy(); c[:, e] = v[0].reshape(128, -1, 4); s[:, e] = v[1]
    return (c.reshape(128, -1), s)
def pk(c, s):
    return (np.ascontiguousarray(c), mx_ref.live(s))
def emit(q):
    return q[0], q[1]
def packed(v, rng):
    q = [mx_ref.quantize(np.ascontiguousarray(v[r])) for r in range(N)]
    return np.stack([a for a, b in q]), np.stack([mx_ref.plane(b, rng) for a, b in q])
def values_of_codes():
    e, c = np.zeros((128, 128, 4), np.float32), np.zeros((128, 2, 4), np.uint8)
    e[np.arange(128), np.arange(128), 0] = 1
    c[:127, :, 0] = np.arange(256).reshape(2, 128).T[:127]
    return mx_ref.matmul(mx_ref.quantize(e.reshape(128, 512).astype(BF)), (c.reshape(128, 8), np.full((16, 2), 127, np.uint8))).T.reshape(-1).astype(np.float64)
CODE_VALUE, SCALE_VALUE = values_of_codes(), 2.0 ** (np.arange(256) - 127.0)
def decode(q):
    return (CODE_VALUE[q[0]].reshape(16, 8, -1, 4) * SCALE_VALUE[q[1]][:, None, :, None] + 0.0).reshape(128, -1).astype(np.float32)
def f(rng, *shape):
    return mx_ref.flush((rng.standard_normal(shape, dtype=np.float32) * np.exp2(rng.integers(-2, 3, shape[:-1] + (1,)))).astype(BF))
def wide(rng, *shape, cols=0):
    v = rng.standard_normal(shape, dtype=np.float32) * np.exp2(rng.integers(-12, 13, shape)).astype(np.float32)
    if cols: v *= np.repeat(np.exp2(rng.integers(-cols, cols + 1, shape[:-2] + (1, shape[-1] // 4))) * (rng.random(shape[:-2] + (1, shape[-1] // 4)) > 0.0625), 4, axis=-1).astype(np.float32)
    return mx_ref.flush(v.astype(BF))
C, A, K = 384, 112, 160
STEP = [1, 2, 3]
MANY = np.repeat(np.array([2, 1, 0]), [A, K, A])
def numbers_of(rng):
    return {"x": np.array(f(rng, N, 128, 4 * C)), "u": np.array(f(rng, N, 128, 512)), "v": np.array(f(rng, N, 128, 512))}
def layers(rng, still=[]):
    w = np.array(f(rng, N, 128, 2048)).reshape(N, 8, 16, 4, 8, 16, 4)
    for i in still:
        w[:, :, i] = 0
        w[:, :, :, :, :, i] = 0
    return w
def weights(rng, w):
    c, p = packed(np.ascontiguousarray(w).reshape(N, 128, 2048), rng)
    return {"wc": c, "ws": p}
def numbers_to(x, u, v):
    return {"x": x.astype(np.float32).reshape(N, 128, 4 * C).astype(BF), "u": u.reshape(N, 128, 512), "v": v}
def setup_inputs(rng):
    return {**numbers_of(rng), **weights(rng, layers(rng))}
def setup_inputs_ties(rng):
    d = numbers_of(rng)
    x = d["x"].astype(np.float32).reshape(N, 8, 16, C, 4)
    x[:, :, 0] = 0
    x[:, :, 0, :, 0] = np.exp2(rng.integers(0, 3, (N, 8, C)))
    u = d["u"].reshape(N, 128, 128, 4)
    u[:, :, ::16] = 0
    o = rng.permutation(N)
    g = rng.permutation(8)[:2]
    for r in range(N):
        for h in range(0, 128, 16): u[r, h, h, 0] = 0.0 if r == o[0] else -1.0 if r == o[1] else 1.0
        if r != o[0] and r ^ 1 != o[0]:
            for i in range(2):
                s = np.ones(C)
                s[A * (r % 2):A * (r % 2) + A] = 0
                s[C - 1 - i * (r % 2)] = 2
                x[r, g[i], 0, :, 0] = np.exp2(2 - s if r == o[1] else s)
    return {**numbers_to(x, u, d["v"]), **weights(rng, layers(rng, [0]))}
def setup_inputs_near(rng):
    d = numbers_of(rng)
    x = d["x"].astype(np.float32).reshape(N, 8, 16, C, 4)
    x[:, :, 0] = 0
    x[:, :, 8:] = 0
    u = d["u"].reshape(N, 128, 128, 4)
    u[:, :, ::16] = 0
    o = rng.permutation(N) % 4
    for r in range(N):
        s = rng.integers(0, 256, (8, C))
        if o[r] < 3:
            for t in range(8): x[r, :, 8 + t // 4, :, t % 4] = ((s >> t) & 1) * 2.0 ** (t - 23)
        if o[r] < 2:
            x[r, :, 0, :, 0] = rng.integers(0, 2, (8, C)) * 2.0 - 1.0
            x[r, :, 11, :, 0] = 2.0 ** -10
        if o[r] == 2:
            for g in range(8): x[r, g, 0, rng.permutation(C)[:2], 0] = np.array([2.0 ** 29, -2.0 ** 29])
        if o[r] == 3:
            x[r, :, 10, :, 0] = rng.integers(-7, 8, (8, C)) * 2.0 ** -30
            for g in rng.permutation(8)[:4]:
                a = rng.permutation(C) % 16
                x[r, g, 10, :, 0] = np.where(a < 8, a + 8, -a) * 2.0 ** -30
                x[r, g, 15, :, 0] = 1.96875 * 2.0 ** -14
        k = 1.0 if o[r] == 0 else 2.0 ** -30
        for h in range(0, 128, 16):
            if o[r] < 2:
                u[r, h, h, 0] = k
                u[r, h + 11, h, 0] = k
            if o[r] == 2: u[r, h, h, 0] = 1.0
            if o[r] < 3: u[r, h + 8:h + 10, h] = k
            else: u[r, h + 10, h, 0] = k
    return {**numbers_to(x, u, d["v"]), **weights(rng, layers(rng, [0, 8, 9, 10, 11, 12, 13, 14, 15]))}
def setup_inputs_huge(rng):
    d = numbers_of(rng)
    h, o = rng.permutation(8), rng.permutation(N)
    x = (0.75 + 0.25 * rng.random((N, 8, 1, C, 1))) * (0.9 + 0.1 * rng.random((N, 8, 16, C, 4))) * 2.0 ** 30
    c = rng.integers(0, 2, (N, 1, 1, C, 1))
    x[:, h[4:6]] *= 0.0625 + 0.9375 * c
    x[:, h[6:]] *= 1.0 - 0.9375 * c
    x[o[0]] = (0.95 + 0.05 * rng.random((8, 16, C, 4))) * 2.0 ** 30
    u = d["u"].reshape(N, 128, 128, 4)
    u[:, :, ::16] = 0
    for r in range(N):
        k = rng.permutation(8)
        for g in range(8):
            e = float(k[g] % 2 * 2 - 1)
            if r == o[0]: u[r, :, 16 * g] = 2.0 ** 30 * e
            else:
                for i in (h[:4] if k[g] < 4 else h[4:]):
                    t = -e if i in h[6:] else e
                    u[r, 16 * i:16 * i + 16, 16 * g] = (2.0 ** 30 * (1 - 0.1 * rng.random((16, 4))) * t).astype(np.float32).astype(BF)
    w = np.zeros((N, 128, 4, 128, 4), np.float32)
    i = np.arange(128)
    for b in range(4): w[:, i, b, i, b] = -4
    return {**numbers_to(x, u, d["v"]), **weights(rng, w.astype(BF))}
def setup_inputs_edges(rng):
    d = numbers_of(rng)
    s = (8, 16, C, 4)
    x = (2 * rng.integers(4, 8, (N,) + s) + 1) * 0.125 * (rng.integers(0, 2, (N,) + s) * 2.0 - 1.0) * np.exp2(rng.integers(-2, 2, (1, 8, 1, C, 1)))
    x[:, :, 0] = 0
    x[:, :, 0, :, 0] = 1.96875 * 2.0 ** 12
    x[:, :, 8:] = 0
    for t in range(9): x[:, :, 8 + t // 4, :, t % 4] = (np.arange(C) >> t) & 1
    u = d["u"].reshape(N, 128, 128, 4)
    u[:, :, ::16] = 0
    w = layers(rng, [0, 8, 9, 10, 11, 12, 13, 14, 15])
    k, e = rng.permutation(8) % N, rng.integers(0, 2, 8)
    for r in range(N):
        for t in range(2):
            c = ((r >> t) & 1) * 2.0 - 1.0
            x[r, :, 11, :, t] = c
            for g in range(8): w[r, g, 11, 0, g, 0, t] = -4096.0 * c
        for g in range(8):
            if (bin(r & int(k[g])).count("1") + int(e[g])) % 2 == 1:
                for t in range(9): u[r, 16 * g + 8 + t // 4, 16 * g, t % 4] = 2.0 ** t
    return {**numbers_to(x, u, d["v"]), **weights(rng, w)}
def setup_inputs_spread(rng):
    d = setup_inputs(rng)
    d["x"] = wide(rng, N, 128, 4 * C, cols=6)
    return d
def check_inputs(d):
    b = []
    for k in ("x", "u", "v"):
        a = np.abs(d[k].astype(np.float32))
        if not (np.isfinite(a).all() and ((a == 0) | (a >= 2.0 ** -30) & (a <= 2.0 ** 30)).all()): b.append("a value of " + k)
    none, least, most = [emit(mx_ref.quantize(np.full((128, 16), k, np.float32).astype(BF)))[1][0, 0] for k in (0.0, 2.0 ** -30, 2.0 ** 30)]
    for r in range(N):
        if ((d["wc"][r] == 0x7F) | (d["wc"][r] == 0xFF)).any(): b.append("wc: a code that is no number")
        s = mx_ref.live(d["ws"][r])
        if ((s != none) & ((s < least) | (s > most))).any(): b.append("ws: a scale out of range")
        if ((s == none)[:, None, :, None] & ((d["wc"][r].reshape(16, 8, -1, 4) & 0x7F) != 0)).any(): b.append("wc: a code that isn't zero beside the scale of zeros")
    return b
def reference(x, u, v, wc, ws):
    qu = [mx_ref.quantize(u[r]) for r in range(N)]
    lay = [pk(wc[r], ws[r]) for r in range(N)]
    now = [x[r] for r in range(N)]
    last = np.zeros((N, 8, C), np.int64)
    for h in STEP:
        own, times_of = [], np.zeros((N, 8, C), np.int64)
        for r in range(N):
            q = mx_ref.quantize(now[r])
            own.append(decode(q).astype(BF))
            s = mx_ref.matmul(qu[r], q)[::16] + np.float32(0.0)
            np.put_along_axis(times_of[r], np.argsort(-s, axis=1, kind="stable"), np.stack([MANY] * 8), axis=1)
        first = np.full((N, 8, C), K)
        part, packs = [], []
        for r in range(N):
            both = np.minimum(times_of[r], times_of[r ^ h])
            e = np.zeros((8, K), np.int64)
            for g in range(8):
                e[g] = np.flatnonzero(both[g])[:K]
                shared = np.repeat(np.arange(C), both[g])
                last[r, g] = np.concatenate([shared, np.repeat(np.arange(C), times_of[r, g] - both[g])])
                first[r, g, np.searchsorted(shared, e[g])] = np.arange(K)
            part.append(gcols(own[r], e))
            packs.append(mx_ref.quantize(part[r]))
        for r in range(N):
            z = mx_ref.quantize((part[r].astype(np.float32) - decode(packs[r ^ h])).astype(BF))
            a = gcols(own[r], last[r]).astype(np.float32)
            made = []
            for b in range(4):
                p = mx_ref.matmul(pick(lay[r], np.arange(128 * b, 128 * b + 128)), z) * np.float32(0.015625)
                made.append(a[:, b::4] + gpick(np.concatenate([p, np.zeros((128, 1), np.float32)], axis=1), first[r]))
            now[r] = tile(made)
    y, nl = np.zeros((N, 128, C), np.float32), np.zeros((N, 8, C), np.float32)
    oc, osc = np.zeros((N, 128, 4 * C), np.uint8), np.zeros((N, 16, C), np.uint8)
    for r in range(N):
        q = mx_ref.quantize(now[r])
        y[r] = mx_ref.matmul(mx_ref.quantize(v[r]), q)
        nl[r] = last[r]
        oc[r], osc[r] = emit(q)
    return {"y": y, "nl": nl, "oc": oc, "osc": osc}

@@ -1,0 +1,335 @@
+from concourse.mybir import dt, AluOpType, ActivationFunctionType
+
+C, A2, K = 384, 112, 160
+NZ = C - A2
+STEP = [1, 2, 3]
+BIG = 2.0 ** 90
+B = 4096.0
+MARK = -2176.0
+TILES = [["d", 23, 22, 21], [20, 19, 18, 17], [16, 15, 14, 13], [12, 11, 10, 9], [8, 7, 6, 5], [4, 3, 2, 1]]
+TN = [384, 320, 256, 192, 128, 128]
+VK = 15
+VORDER = "c1 c2 c3 c4 d0 q5 c5 c6 c7 c8 s1 q4 c9 c10 c11 c12 s2 q0 q3 c13 c14 c15 s3 s4 s5 s6 s7 k0 s8 s9 q1 s10 q2 s11 s12 a13 a14 a15"
+
+F8, U8, BF, F32 = "float8_e4m3fn_x4", "uint8", "bfloat16", "float32"
+SCRATCH = {"ci": ("sbuf", [128, 16], "int32"), "offu": ("sbuf", [128, 8], "uint16"), "off": ("sbuf", [128, 96], "uint16")}
+for _n, _w in [("u", 128), ("u2", 128), ("v", 128), ("w", 512), ("x", 1536), ("xl", 1152), ("e", 512), ("g", 128), ("t", 384), ("z", 160)]:
+    SCRATCH["q" + _n] = ("sbuf", [128, _w], F8)
+    SCRATCH["s" + _n] = ("sbuf", [128, _w], U8)
+for _n, _w in [("x0", 1536), ("xn", 1536), ("ut", 512), ("vt", 512), ("ones", 516), ("eb", 516), ("rg", 512), ("rg2", 512), ("go", 512),
+               ("tt", C), ("cm0", C), ("cmin", C), ("chold", C), ("cx", C), ("keep", C), ("sig", 3 * C), ("ds", C), ("ad", 192), ("adp", 192),
+               ("ha", 400), ("hb", 400), ("pw", 1920), ("bw", 1280), ("ur", C), ("kr", C), ("w", 3072), ("tp", 1536), ("zf", 1536),
+               ("z", 640), ("jk", 1024)]:
+    SCRATCH[_n] = ("sbuf", [128, _w], BF)
+for _n, _w in [("cxk", C), ("cf", 256), ("d1", C), ("pb", C), ("jv", 24 * 128), ("csx", C), ("sa", 256), ("sb", 512), ("ex", NZ), ("ek", C),
+               ("ew", C), ("nlb", C), ("yb", C)]:
+    SCRATCH[_n] = ("sbuf", [128, _w], F32)
+for _m in range(6):
+    SCRATCH["bt%d" % _m] = ("sbuf", [128, 4 * TN[_m]], BF)
+    SCRATCH["qb%d" % _m] = ("sbuf", [128, TN[_m]], F8)
+    SCRATCH["sc%d" % _m] = ("sbuf", [128, TN[_m]], U8)
+for _n in ["pV", "pA", "pC", "pX", "pD0", "pD1", "pD2", "pD3"]:
+    SCRATCH[_n] = ("psum", [128, 512], F32)
+SEMAPHORES = ["cV", "cA", "cP", "cG", "sent"] + ["d%d" % i for i in range(16)] + ["ax%d" % i for i in range(3)] + ["af%d" % i for i in range(3)]
+
+
+def rank_program(g, core, T, topo):
+    rank = T.rank_of(core)
+    if rank is None:
+        return
+    Alu, Act = AluOpType, ActivationFunctionType
+    V, S, P = g.vector, g.scalar, g.tensor
+    queue = {"V": g.vector, "A": g.scalar, "P": g.tensor, "G": g, "S": g.sync}
+    ops, lastw, readers, ndma, sent = [], {}, {}, [0], [0]
+
+    def add(eng, fn, r=(), w=(), kind="c", tok=None, acc=False):
+        deps = set()
+        for k in r:
+            if k in lastw: deps.add(lastw[k])
+            if k.startswith("p_"):
+                deps.update(i for i in readers.get(k, []) if ops[i]["eng"] != eng)
+        for k in w:
+            if k in lastw and not acc: deps.add(lastw[k])
+            deps.update(readers.get(k, []))
+        i = len(ops)
+        if kind == "dma":
+            tok = ("d%d" % ndma[0], 16)
+            ndma[0] += 1
+        ops.append({"eng": eng, "fn": fn, "deps": deps, "kind": kind, "tok": tok})
+        if kind != "remote":
+            for k in r: readers.setdefault(k, []).append(i)
+        for k in w:
+            lastw[k] = i
+            readers[k] = []
+
+    def ts(o, a, s1, s2, op0, op1=None, r=(), w=()):
+        if op1 is None: add("V", lambda: V.tensor_scalar(o, a, s1, None, op0), r, w)
+        else: add("V", lambda: V.tensor_scalar(o, a, s1, s2, op0, op1), r, w)
+    def tt(o, a, b, op, r, w): add("V", lambda: V.tensor_tensor(o, a, b, op), r, w)
+    def scan(o, a, b, init, op0, op1, r, w): add("V", lambda: V.tensor_tensor_scan(o, a, b, init, op0, op1), r, w)
+    def pick(o, a, c, r, w): scan(o, a, c, -2 * B, Alu.max, Alu.add, r, w)
+    def cp(o, a, r, w): add("V", lambda: V.tensor_copy(o, a), r, w)
+    def tr(o, a, r, w): add("V", lambda: V.transpose(o, a), r, w)
+    def fill(o, c, w): add("V", lambda: V.memset(o, c), [], w)
+    def act(o, a, f, r, w, **kw): add("A", lambda: S.activation(o, a, f, **kw), r, w)
+    def qz(c, s, a, r, w): add("V", lambda: V.quantize_mx(c, s, a), r, w)
+    def mm(bank, n, l, x, r, st=True, sp=True):
+        add("P", lambda: P.matmul_mx(T[bank][:, 0:n], l[0], l[1], x[0], x[1], st, sp), r, ["p_" + bank], acc=not st)
+    def dma(e, o, a, r=(), w=()): add(e, lambda: queue[e].dma_start(o, a), r, w, kind="dma")
+    def send(dst, o, a, sem, r):
+        rid, pid, _ = topo.addr(dst)
+        sent[0] += len(topo.engines(core, dst))
+        add("G", lambda: g.remote_dma(o, a, T.sem[sem], T.sem.sent, pid, rid, topo.mask(core, dst)), r, kind="remote")
+    def iota(o, pat, base, cm, w, **kw): add("G", lambda: g.iota(o, pat, base, cm, **kw), [], w)
+    def keys(n, rng=range(4)): return ["%s%d" % (n, i) for i in rng]
+    u8, u32 = dt.uint8, dt.uint32
+
+    dma("A", T.ut[:], T.u[:], w=["ut"])
+    dma("S", T.x0[:, 1024:1536], T.x[:, 1024:1536], w=["x0h"])
+    dma("S", T.x0[:, 0:1024], T.x[:, 0:1024], w=["x0l"])
+    imp = {"allow_small_or_imprecise_dtypes": True}
+    cf = T.cf
+    qc, gq, qa, qb, qd, ng = [cf[:, i:i + 1] for i in range(6)]
+    K16, J, KA, J2, TR, TR2, J3 = [cf[:, 8 + 24 * i:32 + 24 * i] for i in range(7)]
+    val = T.pw[:, 1536:1920]
+    iota(T.ci[:, 0:1], [[0, 1]], 0, 1, ["ci0"])
+    iota(T.tt[:], [[0, 24], [1, 16]], 0, 0, ["tt"], **imp)
+    iota(T.ci[:, 8:16], [[16, 8]], 0, 0, ["ci8"])
+    iota(K16, [[16, 24]], 0, 0, ["K16"], **imp)
+    iota(T.rg[:], [[1, 8], [0, 64]], 0, 0, ["rg"], **imp)
+    fill(T.ones[:], 1.0, ["ones"])
+    add("G", lambda: g.affine_select(T.eb[:], T.ones[:], [[-1, 516]], Alu.is_equal, 0.0, 3, 4), ["ones"], ["eb"])
+    fill(T.ad[:], 0.0, keys("ad", range(3)))
+    ts(T.ci[:, 1:2], T.ci[:, 0:1], 15, None, Alu.bitwise_and, r=["ci0"], w=["ci1"])
+    ts(T.ci[:, 2:3], T.ci[:, 0:1], 4, None, Alu.arith_shift_right, r=["ci0"], w=["ci2"])
+    fill(T.ha[:, 128:144], 0.0, ["haz"])
+    fill(T.hb[:, 128:144], 0.0, ["hbz"])
+    cp(cf[:, 0:2], T.ci[:, 1:3], ["ci1", "ci2"], ["q"])
+    for m in range(6): fill(T["bt%d" % m][:, 64 * TILES[m][3]:4 * TN[m]], 0.0, keys("b%d." % m))
+    ts(qa, qc, 0.5, None, Alu.add, r=["q"], w=["qa"])
+    ts(qb, qc, -0.5, None, Alu.add, r=["q"], w=["qb"])
+    ts(qd, qc, -16.0, None, Alu.add, r=["q"], w=["qd"])
+    ts(ng, gq, -1.0, None, Alu.mult, r=["q"], w=["ng"])
+    ts(T.cm0[:], T.tt[:], qc, 0.5, Alu.is_equal, Alu.subtract, r=["tt", "q"], w=["cm0"])
+    ts(qd, qd, qd, B, Alu.mult, Alu.mult, r=["qd"], w=["qd"])
+    act(T.cmin[:], T.cm0[:], Act.Copy, ["cm0"], ["cmin"], scale=2 * BIG)
+    ts(T.chold[:], T.tt[:], qa, 2 * BIG, Alu.subtract, Alu.mult, r=["tt", "qa"], w=["chold"])
+    ts(T.cx[:], T.tt[:], qb, 2 * B, Alu.subtract, Alu.mult, r=["tt", "qb"], w=["cx"])
+    act(T.keep[:], T.tt[:], Act.Sign, ["tt"], ["keep"])
+    cp(T.offu[:], T.ci[:, 8:16], ["ci8"], ["offu"])
+    fill(T.jv[:, 127:128], 0.0, ["jv0"])
+    for b in range(4): fill(T.w[:, C * b + NZ:C * (b + 1)], 0.0, ["wz%d" % b])
+    ts(T.cx[:, 15:C:16], T.cx[:, 15:C:16], qd, B, Alu.subtract, Alu.subtract, r=["cx", "qd"], w=["cx"])
+    qz(T.qu[:], T.su[:], T.ut[:], ["ut"], ["qu"])
+    cp(T.qu2[:].bitcast(u32), T.qu[:].bitcast(u32).indirect(T.offu[:]), ["qu", "offu"], ["qu2"])
+    cp(T.su2[:], T.su[:].indirect(T.offu[:]), ["qu", "offu"], ["su2"])
+    act(J, K16, Act.Identity, ["K16", "q"], ["J"], bias=qc)
+    act(KA, K16, Act.Identity, ["K16", "q"], ["KA"], bias=qc, scale=-1.0)
+    act(T.rg2[:], T.rg[:], Act.Abs, ["rg", "ng"], ["rg2"], bias=ng)
+    act(KA, KA, Act.Identity, ["KA"], ["KA"], bias=NZ - B - 15.0)
+    act(T.go[:], T.rg2[:], Act.Relu, ["rg2"], ["go"], bias=1.0, scale=-1.0)
+    E = lambda b: (T.qe[:, 128 * b:128 * (b + 1)], T.se[:, 128 * b:128 * (b + 1)])
+
+    place = {}
+    for m in range(6):
+        for t in range(4): place[TILES[m][t]] = (m, t)
+    def plane(k, a, b):
+        m, t = place[k]
+        return T["bt%d" % m][:, 4 * a + t:4 * b:4]
+    pk = lambda k: "b%d.%d" % place[k]
+    piv = lambda k: T.pb[:, 16 * k + 15:16 * k + 16]
+    sumof = lambda k: T.jv[:, 128 * k + 127:128 * k + 128]
+    second = ["pA", "pX", "pV", "pC"]
+    U2 = (T.qu2[:], T.su2[:])
+
+    def blocks(src, skeys, h, key, fill1=None, fill2=None):
+        tr(h[:, 64:128], src, skeys, [key + "t"])
+        if fill1: fill1()
+        scan(h[:, 144:208], T.keep[:, 0:64], h[:, 64:128], 0.0, Alu.mult, Alu.add, [key + "t", "keep"], [key + "p"])
+        scan(h[:, 271:207:-1], h[:, 128:64:-1], T.keep[:, 0:64], 0.0, Alu.add, Alu.mult, [key + "t", key + "z", "keep"], [key + "s"])
+        if fill2: fill2()
+        tr(h[:, 272:400], h[:, 144:272], [key + "p", key + "s"], [key + "d"])
+    def upto(out, h, i, init, key, w):
+        scan(out, h[:, 335 + 32 * i:359 + 32 * i], h[:, 272 + 32 * i:296 + 32 * i], init, Alu.add, Alu.add, [key + "d"], [w])
+
+    sa, sb, ha, hb, off = T.sa, T.sb, T.ha, T.hb, T.off
+    KD, RA, RD, CA, CD, N2, CF, T1, T2 = [sa[:, 24 * i:24 * (i + 1)] for i in range(9)]
+    U1, N3, CS, POS, C2, CM, X1, HB, H, CT, H1, SF = [sb[:, 24 * i:24 * (i + 1)] for i in range(12)]
+    TOT = sb[:, 300:301]
+    oP, oE, oF, oB, oN = off[:, 0:24], off[:, 24:34], off[:, 24:41], off[:, 42:66], off[:, 66:90]
+    wt = lambda b: T.w[:, 1536 + C * b:1536 + C * (b + 1)]
+
+    for rnd in range(4):
+        X, xk = (T.x0, [["x0h"], ["x0l"]]) if rnd == 0 else (T.xn, [keys("xn")] * 2)
+        o = C * rnd
+        QX, qk = (T.qx[:, o:o + C], T.sx[:, o:o + C]), ["qh%d" % rnd, "ql%d" % rnd]
+        if rnd == 3:
+            for i in range(2): qz(T.qx[:, o + 192 * i:o + 192 * (i + 1)], T.sx[:, o + 192 * i:o + 192 * (i + 1)], X[:, 768 * i:768 * (i + 1)], xk[0], [qk[i]])
+            break
+        QH = (T.qx[:, o + 256:o + C], T.sx[:, o + 256:o + C])
+        qz(QH[0], QH[1], X[:, 1024:1536], xk[0], qk[:1])
+        qz(T.qx[:, o:o + 256], T.sx[:, o:o + 256], X[:, 0:1024], xk[1], qk[1:])
+        dst = T.cores[rank ^ STEP[rnd]]
+        ne = len(topo.engines(dst, core))
+        QL = (T.qxl[:, o:o + C], T.sxl[:, o:o + C])
+        mm("pX", 128, U2, QH, ["qu2", "su2", qk[0]])
+        mm("pV", C, U2, QX, ["qu2", "su2"] + qk)
+        mm("pA", C, U2, QX, ["qu2", "su2"] + qk)
+        send(dst, QL[0].bitcast(u8), QX[0].bitcast(u8), "ax%d" % rnd, qk)
+        send(dst, QL[1], QX[1], "ax%d" % rnd, qk)
+        add("-", None, w=["land%d" % rnd], kind="ext", tok=("ax%d" % rnd, 2 * ne))
+        add("-", None, w=["adp%d" % rnd], kind="ext", tok=("af%d" % rnd, ne))
+        if rnd == 0:
+            iota(val, [[1, C]], -128, 0, ["val"], **imp)
+            dma("S", T.qw[:].bitcast(u8), T.wc[:], ["land0"], ["qw"])
+            dma("S", T.sw[:], T.ws[:], w=["sw"])
+            dma("S", T.vt[:], T.v[:], w=["vt"])
+        for lo, hi, n, src, bank in ((256, C, "h", T.pX[:, 0:128], "p_pX"), (0, 256, "l", T.pV[:, 0:256], "p_pV")):
+            tt(T.d1[:, lo:hi], src, T.cmin[:, lo:hi], Alu.min, [bank, "cmin"], ["d1" + n])
+            if rnd == 0 and lo == 0: qz(T.qg[:], T.sg[:], T.go[:], ["go"], ["qg"])
+            scan(T.pb[:, lo:hi], T.chold[:, lo:hi], T.d1[:, lo:hi], -BIG, Alu.min, Alu.max, ["chold", "d1" + n], ["pb" + n])
+        tt(T.bt0[:, 0:4 * C:4], T.pV[:, 0:C], T.pb[:], Alu.is_le, ["p_pV", "pbh", "pbl"], ["b0.0"])
+        ak = list(range(23, VK, -1))
+        for i in range(len(ak) + 1):
+            if i < len(ak):
+                k, s = ak[i], i % 3
+                act(T.sig[:, C * s:C * s + 16 * k], T.pA[:, 0:16 * k], Act.Sign, ["p_pA", "pbh" if k >= 16 else "pbl"], ["sig%d" % s], bias=piv(k), scale=-1.0)
+            if i > 0:
+                k, s = ak[i - 1], (i - 1) % 3
+                act(plane(k, 0, 16 * k), T.sig[:, C * s:C * s + 16 * k], Act.Relu, ["sig%d" % s], [pk(k), "jv%d" % k], accum_out=sumof(k))
+        for st in VORDER.split():
+            k = int(st[1:])
+            if st[0] == "c":
+                ts(plane(k, 0, 16 * k), T.pV[:, 0:16 * k], piv(k), None, Alu.is_lt, r=["p_pV", "pbl"], w=[pk(k)])
+            elif st[0] == "s":
+                scan(T.jv[:, 128 * k + 128 - 8 * k:128 * k + 128], plane(k, 0, 8 * k), plane(k, 8 * k, 16 * k), 0.0, Alu.add, Alu.add, [pk(k)], ["jv%d" % k])
+            elif st[0] == "a":
+                act(T.jk[:, 256 * (k % 4):256 * (k % 4) + 16 * k], plane(k, 0, 16 * k), Act.Copy, [pk(k)], ["jv%d" % k, "jk%d" % (k % 4)], accum_out=sumof(k))
+            elif st[0] == "q":
+                qz(T["qb%d" % k][:], T["sc%d" % k][:], T["bt%d" % k][:], keys("b%d." % k), ["qb%d" % k])
+            elif st[0] == "d":
+                scan(T.ds[:], T.keep[:], T.bt0[:, 0:4 * C:4], 0.0, Alu.mult, Alu.add, ["keep", "b0.0"], ["ds"])
+            else:
+                tt(KD, T.ds[:, 15:C:16], KA, Alu.add, ["ds", "KA"], ["KD"])
+        for i, m in enumerate([0, 5, 4, 3, 1, 2]):
+            mm("pC", TN[m], (T.qg[:], T.sg[:]), (T["qb%d" % m][:], T["sc%d" % m][:]), ["qg", "qb%d" % m], i == 0, i == 5)
+        tt(RA, KD, T.jv[:, 127:24 * 128:128], Alu.add, ["KD"] + keys("jv", range(24)), ["RA"])
+        pick(T.csx[:], T.pC[:, 0:C], T.cx[:], ["p_pC", "cx"], ["csx"])
+        ts(RD, RA, -float(K), None, Alu.add, r=["RA"], w=["RD"])
+        o = 64 * rnd
+        adk = "ad%d" % rnd
+        ak_, dk_ = adk + "a", adk + "d"
+        AD, af, df = T.ad[:, o:o + 64], T.ad[:, o:o + 24], T.ad[:, o + 32:o + 56]
+        tt(af, T.csx[:, 15:C:16], RA, Alu.is_lt, ["csx", "RA", adk], [ak_])
+        tt(df, T.csx[:, 15:C:16], RD, Alu.is_lt, ["csx", "RD", adk], [dk_])
+        send(dst, T.adp[:, o:o + 64], AD, "af%d" % rnd, [ak_, dk_])
+        if rnd == 0:
+            for b in range(4): qz(E(b)[0], E(b)[1], T.eb[:, 3 - b:515 - b], ["eb"], ["qe%d" % b])
+            act(J2, J, Act.Identity, ["J"], ["J2"], bias=float(NZ), scale=2.0)
+            act(J3, J, Act.Identity, ["J"], ["J3"], bias=float(NZ + 2), scale=2.0)
+            act(TR, J, Act.Identity, ["J"], ["TR"], bias=float(C + 1))
+            act(TR2, J, Act.Identity, ["J"], ["TR2"], bias=float(C - 1))
+            act(T.cxk[:], T.cx[:], Act.Copy, ["cx"], ["cxk"])
+            act(T.cxk[:, 15:C:16], T.cx[:, 15:C:16], Act.Identity, ["cx", "cxk"], ["cxk"], bias=-1536.0)
+        for b in range(4): mm("pD%d" % b, C, E(b), QL, ["qe%d" % b, "land%d" % rnd])
+        for b in range(4): act(T.tp[:, b:4 * C:4], T["pD%d" % b][:, 0:C], Act.Copy, ["p_pD%d" % b], ["tp%d" % b], scale=-1.0)
+        for b in range(4): mm(second[b], C, E(b), QX, ["qe%d" % b] + qk)
+        for b in range(4): mm("pD%d" % b, C, E(b), QX, ["qe%d" % b] + qk, True, False)
+        for b in range(4): act(wt(b), T[second[b]][:, 0:C], Act.Copy, ["p_" + second[b]], ["wt%d" % b], scale=64.0)
+        blocks(AD, [ak_, dk_], ha, "ha", lambda: fill(T.bw[:, 0:C], MARK, ["bw"]), lambda: tt(T2, df, TR, Alu.mult, [dk_, "TR"], ["T2"]))
+        tt(T2, TR2, T2, Alu.subtract, ["T2", "TR2"], ["T2"])
+        upto(CA, ha, 0, 0.0, "ha", "CA")
+        upto(CD, ha, 1, 0.0, "ha", "CD")
+        tt(T1, J3, CA, Alu.subtract, ["CA", "J3"], ["T1"])
+        tt(CF, CA, CD, Alu.add, ["CA", "CD"], ["CF"])
+        tt(T1, T1, af, Alu.mult, ["T1", ak_], ["T1"])
+        tt(CF, CF, T2, Alu.add, ["CF", "T2"], ["CF"])
+        tt(N2, J2, T1, Alu.subtract, ["T1", "J2"], ["N2"])
+        qz(T.qt[:], T.st[:], T.tp[:], keys("tp"), ["qt"])
+        for b in range(4): mm("pD%d" % b, C, E(b), (T.qt[:], T.st[:]), ["qe%d" % b, "qt"], False, True)
+        for b in range(4): act(T.zf[:, C * b:C * (b + 1)], T["pD%d" % b][:, 0:C], Act.Copy, ["p_pD%d" % b], ["zf%d" % b])
+        if rnd == 1:
+            fill(T.pw[:, 0:1536], 0.0, ["pw"])
+            qz(T.qv[:], T.sv[:], T.vt[:], ["vt"], ["qv"])
+        sh, m2 = hb[:, 0:24], hb[:, 32:56]
+        tt(hb[:, 0:64], AD, T.adp[:, o:o + 64], Alu.min, [ak_, dk_, "adp%d" % rnd], ["sm"])
+        blocks(hb[:, 0:64], ["sm"], hb, "hb", lambda: ts(U1, sh, -4096.0, None, Alu.mult, r=["sm"], w=["U1"]),
+               lambda: tt(N3, N2, U1, Alu.add, ["U1", "N2"], ["N3"]))
+        ts(HB, m2, -4096.0, 4096.0, Alu.mult, Alu.add, r=["sm"], w=["HB"])
+        scan(sb[:, 287:263:-1], hb[:, 296:272:-1], hb[:, 359:335:-1], 1.0, Alu.add, Alu.add, ["hbd"], ["SF"])
+        upto(CS, hb, 0, -1.0, "hb", "CS")
+        upto(C2, hb, 1, 0.0, "hb", "C2")
+        tt(POS, N3, SF, Alu.add, ["SF", "N3"], ["POS"])
+        tt(CM, CS, C2, Alu.add, ["CS", "C2"], ["CM"])
+        tt(POS, POS, CS, Alu.max, ["CS", "POS"], ["POS"])
+        tt(H, CM, HB, Alu.add, ["CM", "HB"], ["H"])
+        cp(oP, POS, ["POS"], ["oP"])
+        tt(X1, CF, CM, Alu.subtract, ["CF", "CM"], ["X1"])
+        act(sb[:, 320:448], hb[:, 272:400], Act.Copy, ["hbd"], ["TOT"], accum_out=TOT)
+        act(CT, X1, Act.Identity, ["TOT", "X1"], ["CT"], bias=TOT)
+        cp(T.pw[:, 0:1344].indirect(oP), val, ["oP", "val"], ["pw"])
+        tt(H, H, CT, Alu.min, ["H", "CT"], ["H"])
+        pick(T.ex[:], T.pw[:, 0:NZ], T.cx[:, 0:NZ], ["pw", "cx"], ["ex"])
+        cp(oB, H, ["H"], ["oB"])
+        ts(oF, T.ex[:, 15:NZ:16], B + 128, None, Alu.add, r=["ex"], w=["oF"])
+        for b in range(4): act(T.z[:, b:4 * K:4], T.zf[:, C * b:C * (b + 1)].indirect(oE), Act.Copy, ["zf%d" % b, "oF"], ["z%d" % b])
+        cp(T.bw[:].indirect(oB), val, ["oB", "val"], ["bw"])
+        qz(T.qz[:], T.sz[:], T.z[:], keys("z"), ["qz"])
+        for b in (3, 2, 1, 0): act(T.w[:, C * b:C * b + NZ], wt(b).indirect(oF), Act.Copy, ["wt%d" % b, "oF"], ["wg%d" % b])
+        for b in (3, 2, 1, 0):
+            mm(second[b], K, (T.qw[:, 128 * b:128 * (b + 1)], T.sw[:, 128 * b:128 * (b + 1)]), (T.qz[:], T.sz[:]), ["qw", "sw", "qz"])
+        def gsum(b): tt(T.w[:, C * b:C * b + K], T[second[b]][:, 0:K], T.w[:, C * b:C * b + K], Alu.add, ["p_" + second[b], "wg%d" % b], ["wg%d" % b])
+        ts(T.ur[:], T.bw[:, 0:C], MARK, None, Alu.is_equal, r=["bw"], w=["ur"])
+        pick(T.ew[:], T.bw[:, 0:C], T.cx[:], ["bw", "cx"], ["ew"])
+        scan(T.kr[:], T.ones[:, 0:C], T.ur[:], -129.0, Alu.mult, Alu.add, ["ones", "ur"], ["kr"])
+        gsum(3)
+        pick(T.ek[:], T.kr[:], T.cxk[:], ["kr", "cxk"], ["ek"])
+        gsum(2)
+        tt(H1, T.ek[:, 15:C:16], T.ew[:, 15:C:16], Alu.max, ["ek", "ew"], ["H1"])
+        gsum(1)
+        ts(oN, H1, B + 128 + 1536, None, Alu.add, r=["H1"], w=["oN"])
+        gsum(0)
+        def xkeys(b): return ["oN"] + keys("wz") + keys("wg", range(b, 4)) + keys("wt", range(b + 1))
+        win = lambda b: T.w[:, C * b:C * b + 1920].indirect(oN)
+        for b in (3, 2): act(T.xn[:, b:4 * C:4], win(b), Act.Copy, xkeys(b), ["xn%d" % b], scale=1.0 / 64)
+        for b in (1, 0): ts(T.xn[:, b:4 * C:4], win(b), 1.0 / 64, None, Alu.mult, r=xkeys(b), w=["xn%d" % b])
+        if rnd == 2: act(T.nlb[:], T.pw[:].indirect(oN), Act.Identity, ["pw", "val", "oN"], ["nlb"], bias=128.0)
+
+    h, o = C // 2, 3 * C
+    dma("S", T.oc[:], T.qx[:, o:o + C].bitcast(u8), qk)
+    mm("pD0", h, (T.qv[:], T.sv[:]), (T.qx[:, o:o + h], T.sx[:, o:o + h]), ["qv", qk[0]])
+    mm("pD1", h, (T.qv[:], T.sv[:]), (T.qx[:, o + h:o + C], T.sx[:, o + h:o + C]), ["qv", qk[1]])
+    cp(T.yb[:, 0:h], T.pD0[:, 0:h], ["p_pD0"], ["ya"])
+    cp(T.yb[:, h:C], T.pD1[:, 0:h], ["p_pD1"], ["yb"])
+    dma("A", T.nl[:], T.nlb[0:128:16, :], ["nlb"])
+    dma("S", T.y[:, 0:h], T.yb[:, 0:h], ["ya"])
+    dma("A", T.y[:, h:C], T.yb[:, h:C], ["yb"])
+    for k in range(4): dma("S" if k < 2 else "A", T.osc[4 * k:4 * k + 4, :], T.sx[32 * k:32 * k + 4, o:o + C], qk)
+
+    needed = set()
+    for op in ops: needed.update(op["deps"])
+    count = {"V": 0, "A": 0, "P": 0, "G": 0}
+    for i, op in enumerate(ops):
+        if op["kind"] == "c" and i in needed:
+            count[op["eng"]] += 1
+            op["tok"] = ("c" + op["eng"], count[op["eng"]])
+    waited = {e: {} for e in queue}
+    seen = {}
+    for op in ops:
+        if op["kind"] == "ext": continue
+        e = op["eng"]
+        want = {}
+        for d in op["deps"]:
+            s, v = ops[d]["tok"]
+            want[s] = max(want.get(s, 0), v)
+        for s in sorted(want):
+            if waited[e].get(s, 0) < want[s]:
+                queue[e].wait_ge(T.sem[s], want[s])
+                waited[e][s] = want[s]
+                seen[s] = max(seen.get(s, 0), want[s])
+        ins = op["fn"]()
+        if op["kind"] == "dma": ins.then_inc(T.sem[op["tok"][0]], 16)
+        elif op["kind"] == "c" and op["tok"]: ins.then_inc(T.sem[op["tok"][0]], 1)
+    g.wait_ge(T.sem.sent, sent[0])
+    for i in range(ndma[0]):
+        if seen.get("d%d" % i, 0) < 16: g.sync.wait_ge(T.sem["d%d" % i], 16)

@@ -1,36 +1,42 @@
+import numpy as np
 from concourse.mybir import dt, AluOpType, ActivationFunctionType
 
 C, A2, K = 384, 112, 160
 NZ = C - A2
+CP = NZ + 128
 STEP = [1, 2, 3]
 BIG = 2.0 ** 90
 B = 4096.0
-MARK = -2176.0
-TILES = [["d", 23, 22, 21], [20, 19, 18, 17], [16, 15, 14, 13], [12, 11, 10, 9], [8, 7, 6, 5], [4, 3, 2, 1]]
+BL = 1792.0
+MARK = -512.0
+TILES = [["d", 0, 1, 2], [3, 4, 5, 6], [7, 8, 9, 10], [11, 12, 13, 14], [15, 16, 17, 18], [19, 20, 21, 22]]
 TN = [384, 320, 256, 192, 128, 128]
-VK = 15
-VORDER = "c1 c2 c3 c4 d0 q5 c5 c6 c7 c8 s1 q4 c9 c10 c11 c12 s2 q0 q3 c13 c14 c15 s3 s4 s5 s6 s7 k0 s8 s9 q1 s10 q2 s11 s12 a13 a14 a15"
+VK = 6
+MID = 96
+G1, G2, G3, G4 = 128, 200, 128, 200
 
-F8, U8, BF, F32 = "float8_e4m3fn_x4", "uint8", "bfloat16", "float32"
-SCRATCH = {"ci": ("sbuf", [128, 16], "int32"), "offu": ("sbuf", [128, 8], "uint16"), "off": ("sbuf", [128, 96], "uint16")}
-for _n, _w in [("u", 128), ("u2", 128), ("v", 128), ("w", 512), ("x", 1536), ("xl", 1152), ("e", 512), ("g", 128), ("t", 384), ("z", 160)]:
+F8, U8, BF, F32, F16 = "float8_e4m3fn_x4", "uint8", "bfloat16", "float32", "float16"
+SCRATCH = {"ci": ("sbuf", [128, 16], "int32"), "offu": ("sbuf", [128, 8], "uint16"), "off": ("sbuf", [128, 240], "uint16")}
+for _n, _w in [("u", 128), ("u2", 128), ("v", 128), ("w", 512), ("x", 4 * CP), ("xl", 3 * C), ("e", 512), ("g", 128), ("t", C), ("z", K)]:
     SCRATCH["q" + _n] = ("sbuf", [128, _w], F8)
     SCRATCH["s" + _n] = ("sbuf", [128, _w], U8)
-for _n, _w in [("x0", 1536), ("xn", 1536), ("ut", 512), ("vt", 512), ("ones", 516), ("eb", 516), ("rg", 512), ("rg2", 512), ("go", 512),
-               ("tt", C), ("cm0", C), ("cmin", C), ("chold", C), ("cx", C), ("keep", C), ("sig", 3 * C), ("ds", C), ("ad", 192), ("adp", 192),
-               ("ha", 400), ("hb", 400), ("pw", 1920), ("bw", 1280), ("ur", C), ("kr", C), ("w", 3072), ("tp", 1536), ("zf", 1536),
-               ("z", 640), ("jk", 1024)]:
+for _n, _w in [("x0", 4 * CP), ("xn", 4 * CP), ("ut", 512), ("vt", 512), ("ones", 516), ("eb", 516), ("go", 512),
+               ("tt", NZ), ("cm0", NZ), ("cmax", NZ), ("chold", NZ), ("cx", 256), ("c8", 2 * C), ("c16", C), ("keep", NZ), ("sig", NZ * (23 - VK)), ("ds", C),
+               ("ad", 192), ("adp", 192), ("ha", 400), ("hb", 400), ("pw", 1440), ("nw", NZ + C), ("bw", 2320), ("ur", C), ("w", 4 * (NZ + C)), ("tp", 4 * C),
+               ("zf", 4 * C), ("z", 4 * K), ("jb", 192 * VK)]:
     SCRATCH[_n] = ("sbuf", [128, _w], BF)
-for _n, _w in [("cxk", C), ("cf", 256), ("d1", C), ("pb", C), ("jv", 24 * 128), ("csx", C), ("sa", 256), ("sb", 512), ("ex", NZ), ("ek", C),
-               ("ew", C), ("nlb", C), ("yb", C)]:
+for _n, _w in [("cf", 256), ("d1", C), ("pb", C), ("jv", 24), ("csx", C), ("sa", 256), ("sb", 512), ("nlb", C), ("yb", C)]:
     SCRATCH[_n] = ("sbuf", [128, _w], F32)
+for _n, _w in [("ex", NZ), ("ek", 2 * C), ("en", 2 * C)]:
+    SCRATCH[_n] = ("sbuf", [128, _w], F16)
 for _m in range(6):
+    _w = 256 if _m == 3 else TN[_m]
     SCRATCH["bt%d" % _m] = ("sbuf", [128, 4 * TN[_m]], BF)
-    SCRATCH["qb%d" % _m] = ("sbuf", [128, TN[_m]], F8)
-    SCRATCH["sc%d" % _m] = ("sbuf", [128, TN[_m]], U8)
-for _n in ["pV", "pA", "pC", "pX", "pD0", "pD1", "pD2", "pD3"]:
+    SCRATCH["qb%d" % _m] = ("sbuf", [128, _w], F8)
+    SCRATCH["sc%d" % _m] = ("sbuf", [128, _w], U8)
+for _n in ["pV", "pA", "pC0", "pC1", "pD0", "pD1", "pD2", "pD3"]:
     SCRATCH[_n] = ("psum", [128, 512], F32)
-SEMAPHORES = ["cV", "cA", "cP", "cG", "sent"] + ["d%d" % i for i in range(16)] + ["ax%d" % i for i in range(3)] + ["af%d" % i for i in range(3)]
+SEMAPHORES = ["cV", "cA", "cP", "cG", "sent"] + ["d%d" % i for i in range(24)] + ["ax%d" % i for i in range(3)] + ["af%d" % i for i in range(3)]
 
 
 def rank_program(g, core, T, topo):
@@ -40,271 +46,338 @@ def rank_program(g, core, T, topo):
     Alu, Act = AluOpType, ActivationFunctionType
     V, S, P = g.vector, g.scalar, g.tensor
     queue = {"V": g.vector, "A": g.scalar, "P": g.tensor, "G": g, "S": g.sync}
-    ops, lastw, readers, ndma, sent = [], {}, {}, [0], [0]
+    u8, u32 = dt.uint8, dt.uint32
+    ops, lastw, lastr, ndma, sent = [], {}, {}, [0], [0]
+
+    def R(n, a=0, b=None, s=1):
+        w = SCRATCH[n][1][1]
+        if b is None and s > 0: b = w
+        return (n, np.arange(w)[a:b:s], T[n][:, a:b:s], [])
+    def ind(win, off): return (win[0], win[1], win[2].indirect(off[2]), [off])
+    def words(r): return (r[0], r[1], r[2].bitcast(u32), [])
+    def raw(r): return (r[0], r[1], r[2].bitcast(u8), [])
+    def ap(x): return x[2] if isinstance(x, tuple) else x
 
     def add(eng, fn, r=(), w=(), kind="c", tok=None, acc=False):
-        deps = set()
-        for k in r:
-            if k in lastw: deps.add(lastw[k])
-            if k.startswith("p_"):
-                deps.update(i for i in readers.get(k, []) if ops[i]["eng"] != eng)
-        for k in w:
-            if k in lastw and not acc: deps.add(lastw[k])
-            deps.update(readers.get(k, []))
-        i = len(ops)
+        r = [x for x in r if isinstance(x, tuple)]
+        w = [x for x in w if isinstance(x, tuple)]
+        r = r + [o for x in r + w for o in x[3]]
+        i, deps = len(ops), set()
+        who = eng if kind == "c" else i
+        for x in r + w:
+            if x[0] not in lastw: lastw[x[0]], lastr[x[0]] = np.full(SCRATCH[x[0]][1][1], -1), {}
+        def cols(x): return slice(None) if SCRATCH[x[0]][0] == "psum" else x[1]
+        for x in r:
+            deps.update(np.unique(lastw[x[0]][cols(x)]).tolist())
+            if SCRATCH[x[0]][0] == "psum": deps.update(int(a.max()) for e, a in lastr[x[0]].items() if e != who)
+        for x in w:
+            if not acc: deps.update(np.unique(lastw[x[0]][cols(x)]).tolist())
+            deps.update(int(a[cols(x)].max()) for a in lastr[x[0]].values())
+        deps.discard(-1)
         if kind == "dma":
             tok = ("d%d" % ndma[0], 16)
             ndma[0] += 1
         ops.append({"eng": eng, "fn": fn, "deps": deps, "kind": kind, "tok": tok})
         if kind != "remote":
-            for k in r: readers.setdefault(k, []).append(i)
-        for k in w:
-            lastw[k] = i
-            readers[k] = []
+            for x in r: lastr[x[0]].setdefault(who, np.full(SCRATCH[x[0]][1][1], -1))[cols(x)] = i
+        for x in w: lastw[x[0]][cols(x)] = i
 
-    def ts(o, a, s1, s2, op0, op1=None, r=(), w=()):
-        if op1 is None: add("V", lambda: V.tensor_scalar(o, a, s1, None, op0), r, w)
-        else: add("V", lambda: V.tensor_scalar(o, a, s1, s2, op0, op1), r, w)
-    def tt(o, a, b, op, r, w): add("V", lambda: V.tensor_tensor(o, a, b, op), r, w)
-    def scan(o, a, b, init, op0, op1, r, w): add("V", lambda: V.tensor_tensor_scan(o, a, b, init, op0, op1), r, w)
-    def pick(o, a, c, r, w): scan(o, a, c, -2 * B, Alu.max, Alu.add, r, w)
-    def cp(o, a, r, w): add("V", lambda: V.tensor_copy(o, a), r, w)
-    def tr(o, a, r, w): add("V", lambda: V.transpose(o, a), r, w)
-    def fill(o, c, w): add("V", lambda: V.memset(o, c), [], w)
-    def act(o, a, f, r, w, **kw): add("A", lambda: S.activation(o, a, f, **kw), r, w)
-    def qz(c, s, a, r, w): add("V", lambda: V.quantize_mx(c, s, a), r, w)
-    def mm(bank, n, l, x, r, st=True, sp=True):
-        add("P", lambda: P.matmul_mx(T[bank][:, 0:n], l[0], l[1], x[0], x[1], st, sp), r, ["p_" + bank], acc=not st)
-    def dma(e, o, a, r=(), w=()): add(e, lambda: queue[e].dma_start(o, a), r, w, kind="dma")
-    def send(dst, o, a, sem, r):
+    def ts(o, a, s1, s2, op0, op1=None):
+        if op1 is None: add("V", lambda: V.tensor_scalar(o[2], a[2], ap(s1), None, op0), [a, s1], [o])
+        else: add("V", lambda: V.tensor_scalar(o[2], a[2], ap(s1), ap(s2), op0, op1), [a, s1, s2], [o])
+    def tt(o, a, b, op): add("V", lambda: V.tensor_tensor(o[2], a[2], b[2], op), [a, b], [o])
+    def scan(o, a, b, init, op0, op1): add("V", lambda: V.tensor_tensor_scan(o[2], a[2], b[2], init, op0, op1), [a, b], [o])
+    def pick(o, a, c): scan(o, a, c, -2 * B, Alu.max, Alu.add)
+    def cp(o, a): add("V", lambda: V.tensor_copy(o[2], a[2]), [a], [o])
+    def tr(o, a): add("V", lambda: V.transpose(o[2], a[2]), [a], [o])
+    def fill(o, c): add("V", lambda: V.memset(o[2], c), [], [o])
+    def act(o, a, f, **kw): add("A", lambda: S.activation(o[2], a[2], f, **{k: ap(x) for k, x in kw.items()}), [a, kw.get("bias"), kw.get("scale")], [o, kw.get("accum_out")])
+    def Q(n, a=0, b=None): return (R("q" + n, a, b), R("s" + n, a, b))
+    def qz(q, a): add("V", lambda: V.quantize_mx(q[0][2], q[1][2], a[2]), [a], q)
+    def mm(bank, l, x, st=True, sp=True):
+        o = R(bank, 0, len(x[0][1]))
+        add("P", lambda: P.matmul_mx(o[2], l[0][2], l[1][2], x[0][2], x[1][2], st, sp), l + x, [o], acc=not st)
+    def dma(e, o, a): add(e, lambda: queue[e].dma_start(ap(o), ap(a)), [a], [o], kind="dma")
+    def send(dst, o, a, sem):
         rid, pid, _ = topo.addr(dst)
         sent[0] += len(topo.engines(core, dst))
-        add("G", lambda: g.remote_dma(o, a, T.sem[sem], T.sem.sent, pid, rid, topo.mask(core, dst)), r, kind="remote")
-    def iota(o, pat, base, cm, w, **kw): add("G", lambda: g.iota(o, pat, base, cm, **kw), [], w)
-    def keys(n, rng=range(4)): return ["%s%d" % (n, i) for i in rng]
-    u8, u32 = dt.uint8, dt.uint32
+        add("G", lambda: g.remote_dma(o[2], a[2], T.sem[sem], T.sem.sent, pid, rid, topo.mask(core, dst)), [a], kind="remote")
+    def iota(o, pat, base, cm):
+        kw = {} if o[0] == "ci" else {"allow_small_or_imprecise_dtypes": True}
+        add("G", lambda: g.iota(o[2], pat, base, cm, **kw), [], [o])
 
-    dma("A", T.ut[:], T.u[:], w=["ut"])
-    dma("S", T.x0[:, 1024:1536], T.x[:, 1024:1536], w=["x0h"])
-    dma("S", T.x0[:, 0:1024], T.x[:, 0:1024], w=["x0l"])
-    imp = {"allow_small_or_imprecise_dtypes": True}
-    cf = T.cf
-    qc, gq, qa, qb, qd, ng = [cf[:, i:i + 1] for i in range(6)]
-    K16, J, KA, J2, TR, TR2, J3 = [cf[:, 8 + 24 * i:32 + 24 * i] for i in range(7)]
-    val = T.pw[:, 1536:1920]
-    iota(T.ci[:, 0:1], [[0, 1]], 0, 1, ["ci0"])
-    iota(T.tt[:], [[0, 24], [1, 16]], 0, 0, ["tt"], **imp)
-    iota(T.ci[:, 8:16], [[16, 8]], 0, 0, ["ci8"])
-    iota(K16, [[16, 24]], 0, 0, ["K16"], **imp)
-    iota(T.rg[:], [[1, 8], [0, 64]], 0, 0, ["rg"], **imp)
-    fill(T.ones[:], 1.0, ["ones"])
-    add("G", lambda: g.affine_select(T.eb[:], T.ones[:], [[-1, 516]], Alu.is_equal, 0.0, 3, 4), ["ones"], ["eb"])
-    fill(T.ad[:], 0.0, keys("ad", range(3)))
-    ts(T.ci[:, 1:2], T.ci[:, 0:1], 15, None, Alu.bitwise_and, r=["ci0"], w=["ci1"])
-    ts(T.ci[:, 2:3], T.ci[:, 0:1], 4, None, Alu.arith_shift_right, r=["ci0"], w=["ci2"])
-    fill(T.ha[:, 128:144], 0.0, ["haz"])
-    fill(T.hb[:, 128:144], 0.0, ["hbz"])
-    cp(cf[:, 0:2], T.ci[:, 1:3], ["ci1", "ci2"], ["q"])
-    for m in range(6): fill(T["bt%d" % m][:, 64 * TILES[m][3]:4 * TN[m]], 0.0, keys("b%d." % m))
-    ts(qa, qc, 0.5, None, Alu.add, r=["q"], w=["qa"])
-    ts(qb, qc, -0.5, None, Alu.add, r=["q"], w=["qb"])
-    ts(qd, qc, -16.0, None, Alu.add, r=["q"], w=["qd"])
-    ts(ng, gq, -1.0, None, Alu.mult, r=["q"], w=["ng"])
-    ts(T.cm0[:], T.tt[:], qc, 0.5, Alu.is_equal, Alu.subtract, r=["tt", "q"], w=["cm0"])
-    ts(qd, qd, qd, B, Alu.mult, Alu.mult, r=["qd"], w=["qd"])
-    act(T.cmin[:], T.cm0[:], Act.Copy, ["cm0"], ["cmin"], scale=2 * BIG)
-    ts(T.chold[:], T.tt[:], qa, 2 * BIG, Alu.subtract, Alu.mult, r=["tt", "qa"], w=["chold"])
-    ts(T.cx[:], T.tt[:], qb, 2 * B, Alu.subtract, Alu.mult, r=["tt", "qb"], w=["cx"])
-    act(T.keep[:], T.tt[:], Act.Sign, ["tt"], ["keep"])
-    cp(T.offu[:], T.ci[:, 8:16], ["ci8"], ["offu"])
-    fill(T.jv[:, 127:128], 0.0, ["jv0"])
-    for b in range(4): fill(T.w[:, C * b + NZ:C * (b + 1)], 0.0, ["wz%d" % b])
-    ts(T.cx[:, 15:C:16], T.cx[:, 15:C:16], qd, B, Alu.subtract, Alu.subtract, r=["cx", "qd"], w=["cx"])
-    qz(T.qu[:], T.su[:], T.ut[:], ["ut"], ["qu"])
-    cp(T.qu2[:].bitcast(u32), T.qu[:].bitcast(u32).indirect(T.offu[:]), ["qu", "offu"], ["qu2"])
-    cp(T.su2[:], T.su[:].indirect(T.offu[:]), ["qu", "offu"], ["su2"])
-    act(J, K16, Act.Identity, ["K16", "q"], ["J"], bias=qc)
-    act(KA, K16, Act.Identity, ["K16", "q"], ["KA"], bias=qc, scale=-1.0)
-    act(T.rg2[:], T.rg[:], Act.Abs, ["rg", "ng"], ["rg2"], bias=ng)
-    act(KA, KA, Act.Identity, ["KA"], ["KA"], bias=NZ - B - 15.0)
-    act(T.go[:], T.rg2[:], Act.Relu, ["rg2"], ["go"], bias=1.0, scale=-1.0)
-    E = lambda b: (T.qe[:, 128 * b:128 * (b + 1)], T.se[:, 128 * b:128 * (b + 1)])
+    dma("S", R("x0", 4 * NZ, 4 * C), T.x[:, 4 * NZ:4 * C])
+    dma("A", R("ut"), T.u[:])
+    dma("S", R("x0", 512, 4 * NZ), T.x[:, 512:4 * NZ])
+    dma("A", R("x0", 0, 512), T.x[:, 0:512])
+    qc, gq, qa, qr, qd, ng, r4, b4, e4, sF, sN, sH, q17 = [R("cf", i, i + 1) for i in (0, 1, 4, 5, 6, 7, 2, 3, 8, 9, 10, 11, 12)]
+    K16, J, KA, J2, TR, TR2, J3 = [R("cf", 16 + 24 * i, 40 + 24 * i) for i in range(7)]
+    val = R("nw", NZ)
+    ci = lambda a, b: R("ci", a, b)
+    iota(ci(0, 1), [[0, 1]], 0, 1)
+    fill(R("ones"), 1.0)
+    iota(K16, [[16, 24]], 0, 0)
+    iota(R("tt"), [[0, 17], [1, 16]], 0, 0)
+    add("G", lambda: g.affine_select(T.eb[:], T.ones[:], [[-1, 516]], Alu.is_equal, 0.0, 3, 4), [R("ones")], [R("eb")])
+    ts(ci(1, 2), ci(0, 1), 15, None, Alu.bitwise_and)
+    ts(ci(2, 3), ci(0, 1), 0x70, None, Alu.bitwise_and)
+    ts(ci(3, 4), ci(0, 1), 2, 3, Alu.arith_shift_right, Alu.bitwise_and)
+    ts(ci(4, 5), ci(0, 1), 3, None, Alu.bitwise_and)
+    fill(R("x0", 4 * C), 0.0)
+    cp(R("cf", 0, 4), ci(1, 5))
+    cp(R("offu"), R("cf", 16, 24))
+    fill(R("bt5"), 0.0)
+    ts(R("cf", 200, 208), R("cf", 16, 24), gq, None, Alu.is_equal)
+    ts(qa, qc, 0.5, None, Alu.add)
+    qz((R("qb3", 128), R("sc3", 128)), R("bt5"))
+    act(qr, qc, Act.Identity, scale=2 * B, bias=-29 * B)
+    act(qd, qc, Act.Square, bias=1.0)
+    act(J, K16, Act.Identity, bias=qc)
+    for j in range(8): act(R("go", 64 * j, 64 * j + 64), R("ones", 0, 64), Act.Copy, scale=R("cf", 200 + j, 201 + j))
+    for m in range(5): fill(R("bt%d" % m, 4 * (368 - 16 * TILES[m][3])), 0.0)
+    ts(R("cm0"), R("tt"), qc, 0.5, Alu.is_equal, Alu.subtract)
+    ts(R("chold"), R("tt"), qa, -2 * BIG, Alu.subtract, Alu.mult)
+    act(qd, qd, Act.Identity, scale=-B, bias=-B)
+    act(KA, J, Act.Identity, bias=-NZ - B)
+    act(R("cmax"), R("cm0"), Act.Copy, scale=-2 * BIG)
+    act(R("keep"), R("tt"), Act.Sign)
+    act(R("cx"), R("tt", 0, 256), Act.Identity, scale=2 * B, bias=qr)
+    act(R("cf", 64, 64 + VK), R("cf", 64, 64 + VK), Act.Identity, bias=128.0)
+    act(R("cx", 15, 256, 16), R("cx", 15, 256, 16), Act.Identity, bias=qd)
+    for z in (R("jv", 23), R("ad"), R("ha", 128, 144), R("hb", 128, 144), R("xn", 4 * C)): iota(z, [[0, len(z[1])]], 0, 0)
+    E = lambda b: Q("e", 128 * b, 128 * (b + 1))
+    qz(Q("g"), R("go"))
+    ts(R("c8", 0, None, 2), R("ones", 0, C), float(NZ), None, Alu.mult)
+    qz(E(0), R("eb", 3, 515))
+    qz(Q("u"), R("ut"))
+    act(R("su2"), ind(R("su"), R("offu")), Act.Copy)
+    cp(words(R("qu2")), ind(words(R("qu")), R("offu")))
+    act(sH, r4, Act.Identity, scale=-2 * BL, bias=BL)
+    act(e4, r4, Act.Square, bias=-4.0)
+    act(sF, b4, Act.Identity, bias=4 * (BL + 128))
+    act(R("cf", 208, 212), R("tt", 0, 4), Act.Identity, scale=2 * BL, bias=sH)
+    act(e4, e4, Act.Identity, scale=-BL, bias=-BL)
+    act(sN, r4, Act.Identity, scale=4.0 * NZ, bias=sF)
+    act(R("cf", 211, 212), R("cf", 211, 212), Act.Identity, bias=e4)
+    act(sN, sN, Act.Identity, bias=-12.0 * NZ)
+    for t in range(4): act(R("c8", 2 * t + 1, None, 8), R("ones", 0, 96), Act.Copy, scale=R("cf", 208 + t, 209 + t))
+    act(sH, sN, Act.Identity, bias=-4.0 * K)
+    U2 = Q("u2")
 
     place = {}
     for m in range(6):
         for t in range(4): place[TILES[m][t]] = (m, t)
     def plane(k, a, b):
         m, t = place[k]
-        return T["bt%d" % m][:, 4 * a + t:4 * b:4]
-    pk = lambda k: "b%d.%d" % place[k]
-    piv = lambda k: T.pb[:, 16 * k + 15:16 * k + 16]
-    sumof = lambda k: T.jv[:, 128 * k + 127:128 * k + 128]
-    second = ["pA", "pX", "pV", "pC"]
-    U2 = (T.qu2[:], T.su2[:])
+        return R("bt%d" % m, 4 * a + t, 4 * b, 4)
+    def back(k, a, b):
+        m, t = place[k]
+        return R("bt%d" % m, 4 * (C - 1 - a) + t, 4 * (C - 1 - b) + t if b < C else None, -4)
+    piv = lambda k: R("pb", 16 * k + 15, 16 * k + 16)
+    second = ["pV", "pA", "pC1", "pC0"]
+    sig = lambda k: R("sig", NZ * (k - VK), NZ * (k - VK) + 368 - 16 * k)
+    def relu(k): act(back(k, 16 * k + 16, C), sig(k), Act.Relu, scale=-1.0, accum_out=R("jv", k, k + 1))
+    def sign(k): act(sig(k), R("pD1", 16 * k + 16 - NZ, A2) if 16 * k >= NZ else R("pA", 16 * k + 16, C), Act.Sign, bias=piv(k), scale=-1.0)
+    def signs(ks, lag):
+        for i in range(len(ks) + lag):
+            if i < len(ks): sign(ks[i])
+            if i >= lag: relu(ks[i - lag])
+    def hold(lo, hi, src, between=None):
+        tt(R("d1", lo, hi), src, R("cmax", 0, hi - lo), Alu.max)
+        if between: between()
+        scan(R("pb", lo, hi), R("chold", 0, hi - lo), R("d1", lo, hi), 0.0, Alu.max, Alu.min)
+    def within(lo, hi, src, between=None):
+        tt(back("d", lo, hi), src, R("pb", lo, hi), Alu.is_gt)
+        if between: between()
+        scan(R("ds", C - hi, C - lo), R("keep", 0, hi - lo), plane("d", C - hi, C - lo), 0.0, Alu.mult, Alu.add)
 
-    def blocks(src, skeys, h, key, fill1=None, fill2=None):
-        tr(h[:, 64:128], src, skeys, [key + "t"])
-        if fill1: fill1()
-        scan(h[:, 144:208], T.keep[:, 0:64], h[:, 64:128], 0.0, Alu.mult, Alu.add, [key + "t", "keep"], [key + "p"])
-        scan(h[:, 271:207:-1], h[:, 128:64:-1], T.keep[:, 0:64], 0.0, Alu.add, Alu.mult, [key + "t", key + "z", "keep"], [key + "s"])
-        if fill2: fill2()
-        tr(h[:, 272:400], h[:, 144:272], [key + "p", key + "s"], [key + "d"])
-    def upto(out, h, i, init, key, w):
-        scan(out, h[:, 335 + 32 * i:359 + 32 * i], h[:, 272 + 32 * i:296 + 32 * i], init, Alu.add, Alu.add, [key + "d"], [w])
+    def blocks(src, h, fill1, fill2):
+        tr(R(h, 64, 128), src)
+        fill1()
+        scan(R(h, 144, 208), R("keep", 0, 64), R(h, 64, 128), 0.0, Alu.mult, Alu.add)
+        scan(R(h, 271, 207, -1), R(h, 128, 64, -1), R("keep", 0, 64), 0.0, Alu.add, Alu.mult)
+        fill2()
+        tr(R(h, 272, 400), R(h, 144, 272))
+    def upto(out, h, i, init): scan(out, R(h, 335 + 32 * i, 359 + 32 * i), R(h, 272 + 32 * i, 296 + 32 * i), init, Alu.add, Alu.add)
 
-    sa, sb, ha, hb, off = T.sa, T.sb, T.ha, T.hb, T.off
-    KD, RA, RD, CA, CD, N2, CF, T1, T2 = [sa[:, 24 * i:24 * (i + 1)] for i in range(9)]
-    U1, N3, CS, POS, C2, CM, X1, HB, H, CT, H1, SF = [sb[:, 24 * i:24 * (i + 1)] for i in range(12)]
-    TOT = sb[:, 300:301]
-    oP, oE, oF, oB, oN = off[:, 0:24], off[:, 24:34], off[:, 24:41], off[:, 42:66], off[:, 66:90]
-    wt = lambda b: T.w[:, 1536 + C * b:1536 + C * (b + 1)]
+    KD, RA, RD, CA, CD, N2, CF, T1 = [R("sa", 24 * i, 24 * (i + 1)) for i in range(8)]
+    U1, N3, CS, POS, C2, CM, X1, HB, H, CT, H1, SF = [R("sb", 24 * i, 24 * (i + 1)) for i in range(12)]
+    T2 = R("sb", 448, 472)
+    TOT = R("sb", 300, 301)
+    oP, oB, oL = R("off", 0, 24), R("off", 24, 48), R("off", 48, 72)
+    oF = lambda a, b: R("off", 72 + a // 4, 72 + b // 4)
+    oN = lambda a, b: R("off", 140 + a // 4, 140 + b // 4)
+    state = lambda rnd: "x0" if rnd == 0 else "xn"
+    def pack(rnd, a, b): qz(Q("x", CP * rnd + a, CP * rnd + b), R(state(rnd), 4 * a, 4 * b))
+    def high(rnd):
+        pack(rnd, NZ, CP)
+        if rnd < 3:
+            for bank in ("pD0", "pD1"): mm(bank, U2, Q("x", CP * rnd + NZ, CP * (rnd + 1)))
 
-    for rnd in range(4):
-        X, xk = (T.x0, [["x0h"], ["x0l"]]) if rnd == 0 else (T.xn, [keys("xn")] * 2)
-        o = C * rnd
-        QX, qk = (T.qx[:, o:o + C], T.sx[:, o:o + C]), ["qh%d" % rnd, "ql%d" % rnd]
-        if rnd == 3:
-            for i in range(2): qz(T.qx[:, o + 192 * i:o + 192 * (i + 1)], T.sx[:, o + 192 * i:o + 192 * (i + 1)], X[:, 768 * i:768 * (i + 1)], xk[0], [qk[i]])
-            break
-        QH = (T.qx[:, o + 256:o + C], T.sx[:, o + 256:o + C])
-        qz(QH[0], QH[1], X[:, 1024:1536], xk[0], qk[:1])
-        qz(T.qx[:, o:o + 256], T.sx[:, o:o + 256], X[:, 0:1024], xk[1], qk[1:])
+    high(0)
+    qz(E(1), R("eb", 2, 514))
+    for rnd in range(3):
+        QX, QL = Q("x", CP * rnd, CP * rnd + C), Q("xl", C * rnd, C * (rnd + 1))
         dst = T.cores[rank ^ STEP[rnd]]
         ne = len(topo.engines(dst, core))
-        QL = (T.qxl[:, o:o + C], T.sxl[:, o:o + C])
-        mm("pX", 128, U2, QH, ["qu2", "su2", qk[0]])
-        mm("pV", C, U2, QX, ["qu2", "su2"] + qk)
-        mm("pA", C, U2, QX, ["qu2", "su2"] + qk)
-        send(dst, QL[0].bitcast(u8), QX[0].bitcast(u8), "ax%d" % rnd, qk)
-        send(dst, QL[1], QX[1], "ax%d" % rnd, qk)
-        add("-", None, w=["land%d" % rnd], kind="ext", tok=("ax%d" % rnd, 2 * ne))
-        add("-", None, w=["adp%d" % rnd], kind="ext", tok=("af%d" % rnd, ne))
+        hold(NZ, C, R("pD0", 0, A2), lambda: pack(rnd, 128, NZ))
+        pack(rnd, 0, 128)
+        for bank in ("pV", "pA"): mm(bank, U2, QX)
+        send(dst, raw(QL[0]), raw(QX[0]), "ax%d" % rnd)
+        send(dst, QL[1], QX[1], "ax%d" % rnd)
+        add("-", None, w=QL, kind="ext", tok=("ax%d" % rnd, 2 * ne))
+        add("-", None, w=[R("adp", 64 * rnd, 64 * rnd + 64)], kind="ext", tok=("af%d" % rnd, ne))
+        signs(list(range(22, 16, -1)), 5)
         if rnd == 0:
-            iota(val, [[1, C]], -128, 0, ["val"], **imp)
-            dma("S", T.qw[:].bitcast(u8), T.wc[:], ["land0"], ["qw"])
-            dma("S", T.sw[:], T.ws[:], w=["sw"])
-            dma("S", T.vt[:], T.v[:], w=["vt"])
-        for lo, hi, n, src, bank in ((256, C, "h", T.pX[:, 0:128], "p_pX"), (0, 256, "l", T.pV[:, 0:256], "p_pV")):
-            tt(T.d1[:, lo:hi], src, T.cmin[:, lo:hi], Alu.min, [bank, "cmin"], ["d1" + n])
-            if rnd == 0 and lo == 0: qz(T.qg[:], T.sg[:], T.go[:], ["go"], ["qg"])
-            scan(T.pb[:, lo:hi], T.chold[:, lo:hi], T.d1[:, lo:hi], -BIG, Alu.min, Alu.max, ["chold", "d1" + n], ["pb" + n])
-        tt(T.bt0[:, 0:4 * C:4], T.pV[:, 0:C], T.pb[:], Alu.is_le, ["p_pV", "pbh", "pbl"], ["b0.0"])
-        ak = list(range(23, VK, -1))
-        for i in range(len(ak) + 1):
-            if i < len(ak):
-                k, s = ak[i], i % 3
-                act(T.sig[:, C * s:C * s + 16 * k], T.pA[:, 0:16 * k], Act.Sign, ["p_pA", "pbh" if k >= 16 else "pbl"], ["sig%d" % s], bias=piv(k), scale=-1.0)
-            if i > 0:
-                k, s = ak[i - 1], (i - 1) % 3
-                act(plane(k, 0, 16 * k), T.sig[:, C * s:C * s + 16 * k], Act.Relu, ["sig%d" % s], [pk(k), "jv%d" % k], accum_out=sumof(k))
-        for st in VORDER.split():
-            k = int(st[1:])
-            if st[0] == "c":
-                ts(plane(k, 0, 16 * k), T.pV[:, 0:16 * k], piv(k), None, Alu.is_lt, r=["p_pV", "pbl"], w=[pk(k)])
-            elif st[0] == "s":
-                scan(T.jv[:, 128 * k + 128 - 8 * k:128 * k + 128], plane(k, 0, 8 * k), plane(k, 8 * k, 16 * k), 0.0, Alu.add, Alu.add, [pk(k)], ["jv%d" % k])
-            elif st[0] == "a":
-                act(T.jk[:, 256 * (k % 4):256 * (k % 4) + 16 * k], plane(k, 0, 16 * k), Act.Copy, [pk(k)], ["jv%d" % k, "jk%d" % (k % 4)], accum_out=sumof(k))
-            elif st[0] == "q":
-                qz(T["qb%d" % k][:], T["sc%d" % k][:], T["bt%d" % k][:], keys("b%d." % k), ["qb%d" % k])
-            elif st[0] == "d":
-                scan(T.ds[:], T.keep[:], T.bt0[:, 0:4 * C:4], 0.0, Alu.mult, Alu.add, ["keep", "b0.0"], ["ds"])
-            else:
-                tt(KD, T.ds[:, 15:C:16], KA, Alu.add, ["ds", "KA"], ["KD"])
-        for i, m in enumerate([0, 5, 4, 3, 1, 2]):
-            mm("pC", TN[m], (T.qg[:], T.sg[:]), (T["qb%d" % m][:], T["sc%d" % m][:]), ["qg", "qb%d" % m], i == 0, i == 5)
-        tt(RA, KD, T.jv[:, 127:24 * 128:128], Alu.add, ["KD"] + keys("jv", range(24)), ["RA"])
-        pick(T.csx[:], T.pC[:, 0:C], T.cx[:], ["p_pC", "cx"], ["csx"])
-        ts(RD, RA, -float(K), None, Alu.add, r=["RA"], w=["RD"])
+            iota(val, [[1, C]], -128, 0)
+            add("S", lambda: g.sync.dma_start(T.qw[:].bitcast(u8), T.wc[:]), QL, [R("qw")], kind="dma")
+            dma("S", R("vt"), T.v[:])
+            dma("S", R("sw"), T.ws[:])
+        within(NZ, C, R("pD0", 0, A2))
+        hold(MID, NZ, R("pV", MID, NZ), lambda: tt(R("d1", 0, MID), R("pV", 0, MID), R("cmax", 0, MID), Alu.max))
+        scan(R("pb", 0, MID), R("chold", 0, MID), R("d1", 0, MID), 0.0, Alu.max, Alu.min)
+        signs(list(range(VK, 17)), 2)
+        G = Q("g")
+        def tile(m):
+            q = lambda a, b: (R("qb%d" % m, a, b), R("sc%d" % m, a, b))
+            qz(q(0, TN[m]), R("bt%d" % m, 0, 4 * TN[m]))
+            mm("pC0", G, q(0, 128), m == 5, m == 4)
+            if m < 4: mm("pC1", G, q(128, max(256, TN[m])), m == 0, m == 3)
+        def compare(k): ts(back(k, 16 * k + 16, C), R("pV", 16 * k + 16, C), piv(k), None, Alu.is_gt)
+        def rows(k):
+            n = 184 - 8 * k
+            scan(R("jb", 192 * k + 192 - n, 192 * k + 192), plane(k, 0, n), plane(k, n, 2 * n), -128.0, Alu.add, Alu.add)
+        within(0, NZ, R("pV", 0, NZ), lambda: tile(5))
+        for k in range(3): compare(k)
+        rows(0)
+        tile(0)
+        for k in range(3, VK): compare(k)
+        tt(KD, R("ds", C - 1, None, -16), KA, Alu.add)
+        def theirs(*bs):
+            for b in bs:
+                if rnd > 0: mm("pD%d" % b, E(b), QL)
+        rows(1)
+        rows(2)
+        tile(1)
+        theirs(0)
+        for k in range(3, VK): rows(k)
+        tile(2)
+        theirs(1)
+        tile(3)
+        tile(4)
+        theirs(2, 3)
+        tt(R("sa", 24, 24 + VK), R("sa", 0, VK), R("jb", 191, None, 192), Alu.add)
+        tt(R("sa", 24 + VK, 48), R("sa", VK, 24), R("jv", VK, 24), Alu.add)
+        fill(R("bw", 0, 2 * C), MARK)
+        pick(R("csx", 128, C), R("pC1", 0, 256), R("cx"))
+        pick(R("csx", 0, 128), R("pC0", 0, 128), R("cx", 0, 128))
+        ts(RD, RA, float(K), None, Alu.add)
         o = 64 * rnd
-        adk = "ad%d" % rnd
-        ak_, dk_ = adk + "a", adk + "d"
-        AD, af, df = T.ad[:, o:o + 64], T.ad[:, o:o + 24], T.ad[:, o + 32:o + 56]
-        tt(af, T.csx[:, 15:C:16], RA, Alu.is_lt, ["csx", "RA", adk], [ak_])
-        tt(df, T.csx[:, 15:C:16], RD, Alu.is_lt, ["csx", "RD", adk], [dk_])
-        send(dst, T.adp[:, o:o + 64], AD, "af%d" % rnd, [ak_, dk_])
+        AD, af, df = R("ad", o, o + 64), R("ad", o, o + 24), R("ad", o + 32, o + 56)
+        tt(af, R("csx", C - 1, None, -16), RA, Alu.is_gt)
+        tt(df, R("csx", C - 1, None, -16), RD, Alu.is_gt)
+        send(dst, R("adp", o, o + 64), AD, "af%d" % rnd)
         if rnd == 0:
-            for b in range(4): qz(E(b)[0], E(b)[1], T.eb[:, 3 - b:515 - b], ["eb"], ["qe%d" % b])
-            act(J2, J, Act.Identity, ["J"], ["J2"], bias=float(NZ), scale=2.0)
-            act(J3, J, Act.Identity, ["J"], ["J3"], bias=float(NZ + 2), scale=2.0)
-            act(TR, J, Act.Identity, ["J"], ["TR"], bias=float(C + 1))
-            act(TR2, J, Act.Identity, ["J"], ["TR2"], bias=float(C - 1))
-            act(T.cxk[:], T.cx[:], Act.Copy, ["cx"], ["cxk"])
-            act(T.cxk[:, 15:C:16], T.cx[:, 15:C:16], Act.Identity, ["cx", "cxk"], ["cxk"], bias=-1536.0)
-        for b in range(4): mm("pD%d" % b, C, E(b), QL, ["qe%d" % b, "land%d" % rnd])
-        for b in range(4): act(T.tp[:, b:4 * C:4], T["pD%d" % b][:, 0:C], Act.Copy, ["p_pD%d" % b], ["tp%d" % b], scale=-1.0)
-        for b in range(4): mm(second[b], C, E(b), QX, ["qe%d" % b] + qk)
-        for b in range(4): mm("pD%d" % b, C, E(b), QX, ["qe%d" % b] + qk, True, False)
-        for b in range(4): act(wt(b), T[second[b]][:, 0:C], Act.Copy, ["p_" + second[b]], ["wt%d" % b], scale=64.0)
-        blocks(AD, [ak_, dk_], ha, "ha", lambda: fill(T.bw[:, 0:C], MARK, ["bw"]), lambda: tt(T2, df, TR, Alu.mult, [dk_, "TR"], ["T2"]))
-        tt(T2, TR2, T2, Alu.subtract, ["T2", "TR2"], ["T2"])
-        upto(CA, ha, 0, 0.0, "ha", "CA")
-        upto(CD, ha, 1, 0.0, "ha", "CD")
-        tt(T1, J3, CA, Alu.subtract, ["CA", "J3"], ["T1"])
-        tt(CF, CA, CD, Alu.add, ["CA", "CD"], ["CF"])
-        tt(T1, T1, af, Alu.mult, ["T1", ak_], ["T1"])
-        tt(CF, CF, T2, Alu.add, ["CF", "T2"], ["CF"])
-        tt(N2, J2, T1, Alu.subtract, ["T1", "J2"], ["N2"])
-        qz(T.qt[:], T.st[:], T.tp[:], keys("tp"), ["qt"])
-        for b in range(4): mm("pD%d" % b, C, E(b), (T.qt[:], T.st[:]), ["qe%d" % b, "qt"], False, True)
-        for b in range(4): act(T.zf[:, C * b:C * (b + 1)], T["pD%d" % b][:, 0:C], Act.Copy, ["p_pD%d" % b], ["zf%d" % b])
+            for b in (2, 3): qz(E(b), R("eb", 3 - b, 515 - b))
+            act(J2, J, Act.Identity, bias=float(NZ), scale=2.0)
+            act(TR2, J, Act.Identity, bias=float(C - 1))
+            for b in range(4): mm("pD%d" % b, E(b), QL)
+        for b in range(4): act(R("tp", b, None, 4), R("pD%d" % b, 0, C), Act.Copy, scale=-1.0)
+        for b in range(4): mm(second[b], E(b), QX)
+        for b in range(4): mm("pD%d" % b, E(b), QX, True, False)
+        for b in range(4): act(R("w", 4 * NZ + b, None, 4), R(second[b], 0, C), Act.Copy, scale=64.0)
+        def spare():
+            if rnd == 1:
+                qz(Q("v"), R("vt"))
+                ts(q17, qc, -17.0, BL, Alu.add, Alu.mult)
+            if rnd == 2: ts(R("c16"), R("c16"), 2 * BL, None, Alu.mult)
+        blocks(AD, "ha", lambda: ts(R("sa", 192, 256), AD, -4096.0, 4094.0, Alu.mult, Alu.add), spare)
+        qz(Q("t"), R("tp"))
+        for b in range(4): mm("pD%d" % b, E(b), Q("t"), False, True)
+        def diff(b): act(R("zf", b, None, 4), R("pD%d" % b, 0, C), Act.Copy)
+        for b in range(3): diff(b)
+        upto(CA, "ha", 0, 0.0)
+        upto(CD, "ha", 1, 0.0)
+        tt(T2, R("sa", 224, 248), TR2, Alu.min)
+        sh, m2 = R("hb", 0, 24), R("hb", 32, 56)
+        tt(R("hb", 0, 64), AD, R("adp", o, o + 64), Alu.min)
+        tt(T1, CA, R("sa", 192, 216), Alu.add)
+        tt(CF, CA, CD, Alu.add)
+        def fill1():
+            ts(U1, sh, -4096.0, None, Alu.mult)
+            tt(N2, J2, T1, Alu.min)
+            tt(CF, CF, T2, Alu.add)
+            ts(HB, m2, -4096.0, 4096.0, Alu.mult, Alu.add)
+        blocks(R("hb", 0, 64), "hb", fill1, lambda: tt(N3, N2, U1, Alu.add))
         if rnd == 1:
-            fill(T.pw[:, 0:1536], 0.0, ["pw"])
-            qz(T.qv[:], T.sv[:], T.vt[:], ["vt"], ["qv"])
-        sh, m2 = hb[:, 0:24], hb[:, 32:56]
-        tt(hb[:, 0:64], AD, T.adp[:, o:o + 64], Alu.min, [ak_, dk_, "adp%d" % rnd], ["sm"])
-        blocks(hb[:, 0:64], ["sm"], hb, "hb", lambda: ts(U1, sh, -4096.0, None, Alu.mult, r=["sm"], w=["U1"]),
-               lambda: tt(N3, N2, U1, Alu.add, ["U1", "N2"], ["N3"]))
-        ts(HB, m2, -4096.0, 4096.0, Alu.mult, Alu.add, r=["sm"], w=["HB"])
-        scan(sb[:, 287:263:-1], hb[:, 296:272:-1], hb[:, 359:335:-1], 1.0, Alu.add, Alu.add, ["hbd"], ["SF"])
-        upto(CS, hb, 0, -1.0, "hb", "CS")
-        upto(C2, hb, 1, 0.0, "hb", "C2")
-        tt(POS, N3, SF, Alu.add, ["SF", "N3"], ["POS"])
-        tt(CM, CS, C2, Alu.add, ["CS", "C2"], ["CM"])
-        tt(POS, POS, CS, Alu.max, ["CS", "POS"], ["POS"])
-        tt(H, CM, HB, Alu.add, ["CM", "HB"], ["H"])
-        cp(oP, POS, ["POS"], ["oP"])
-        tt(X1, CF, CM, Alu.subtract, ["CF", "CM"], ["X1"])
-        act(sb[:, 320:448], hb[:, 272:400], Act.Copy, ["hbd"], ["TOT"], accum_out=TOT)
-        act(CT, X1, Act.Identity, ["TOT", "X1"], ["CT"], bias=TOT)
-        cp(T.pw[:, 0:1344].indirect(oP), val, ["oP", "val"], ["pw"])
-        tt(H, H, CT, Alu.min, ["H", "CT"], ["H"])
-        pick(T.ex[:], T.pw[:, 0:NZ], T.cx[:, 0:NZ], ["pw", "cx"], ["ex"])
-        cp(oB, H, ["H"], ["oB"])
-        ts(oF, T.ex[:, 15:NZ:16], B + 128, None, Alu.add, r=["ex"], w=["oF"])
-        for b in range(4): act(T.z[:, b:4 * K:4], T.zf[:, C * b:C * (b + 1)].indirect(oE), Act.Copy, ["zf%d" % b, "oF"], ["z%d" % b])
-        cp(T.bw[:].indirect(oB), val, ["oB", "val"], ["bw"])
-        qz(T.qz[:], T.sz[:], T.z[:], keys("z"), ["qz"])
-        for b in (3, 2, 1, 0): act(T.w[:, C * b:C * b + NZ], wt(b).indirect(oF), Act.Copy, ["wt%d" % b, "oF"], ["wg%d" % b])
-        for b in (3, 2, 1, 0):
-            mm(second[b], K, (T.qw[:, 128 * b:128 * (b + 1)], T.sw[:, 128 * b:128 * (b + 1)]), (T.qz[:], T.sz[:]), ["qw", "sw", "qz"])
-        def gsum(b): tt(T.w[:, C * b:C * b + K], T[second[b]][:, 0:K], T.w[:, C * b:C * b + K], Alu.add, ["p_" + second[b], "wg%d" % b], ["wg%d" % b])
-        ts(T.ur[:], T.bw[:, 0:C], MARK, None, Alu.is_equal, r=["bw"], w=["ur"])
-        pick(T.ew[:], T.bw[:, 0:C], T.cx[:], ["bw", "cx"], ["ew"])
-        scan(T.kr[:], T.ones[:, 0:C], T.ur[:], -129.0, Alu.mult, Alu.add, ["ones", "ur"], ["kr"])
-        gsum(3)
-        pick(T.ek[:], T.kr[:], T.cxk[:], ["kr", "cxk"], ["ek"])
-        gsum(2)
-        tt(H1, T.ek[:, 15:C:16], T.ew[:, 15:C:16], Alu.max, ["ek", "ew"], ["H1"])
-        gsum(1)
-        ts(oN, H1, B + 128 + 1536, None, Alu.add, r=["H1"], w=["oN"])
+            for a in (0, 192): ts(R("c16", a, a + 192), R("tt", 0, 192), qc, 0.5, Alu.is_ge, Alu.subtract)
+        if rnd == 2: ts(R("c16", 15, None, 16), R("c16", 15, None, 16), q17, None, Alu.add)
+        scan(R("sb", 287, 263, -1), R("hb", 296, 272, -1), R("hb", 359, 335, -1), 1.0, Alu.add, Alu.add)
+        upto(CS, "hb", 0, -1.0)
+        upto(C2, "hb", 1, 0.0)
+        tt(POS, N3, SF, Alu.add)
+        tt(CM, CS, C2, Alu.add)
+        tt(POS, POS, CS, Alu.max)
+        tt(X1, CF, CM, Alu.subtract)
+        tt(H, CM, HB, Alu.add)
+        cp(oP, POS)
+        act(R("sb", 320, 448), R("hb", 272, 400), Act.Copy, accum_out=TOT)
+        diff(3)
+        act(CT, X1, Act.Identity, bias=TOT)
+        cp(ind(R("pw"), oP), val)
+        tt(H, H, CT, Alu.min)
+        pick(R("ex"), R("pw", 0, NZ), R("c8", 1, 2 * NZ, 2))
+        ts(oB, H, 2.0, None, Alu.mult)
+        ts(oF(0, NZ), R("ex", 3, None, 4), 4.0, sF, Alu.mult, Alu.add)
+        if rnd == 2: act(R("nw", 0, NZ), R("pw", 0, NZ), Act.Copy)
+        T64 = R("w", 4 * NZ)
+        act(R("z"), ind(R("zf"), oF(0, K)), Act.Copy)
+        cp(ind(R("bw"), oB), val)
+        qz(Q("z"), R("z"))
+        act(R("w", 0, 4 * K), ind(T64, oF(0, K)), Act.Copy)
+        act(R("w", 4 * K, 4 * NZ), ind(T64, oF(K, NZ)), Act.Copy)
+        for b in range(4): mm(second[b], Q("w", 128 * b, 128 * (b + 1)), Q("z"))
+        def gsum(b): tt(R("w", b, 4 * K, 4), R(second[b], 0, K), R("w", b, 4 * K, 4), Alu.add)
+        ts(R("ur"), R("bw", 0, 2 * C, 2), MARK, None, Alu.is_equal)
+        scan(R("bw", 1, 2 * C, 2), R("ones", 0, C), R("ur"), -129.0, Alu.mult, Alu.add)
         gsum(0)
-        def xkeys(b): return ["oN"] + keys("wz") + keys("wg", range(b, 4)) + keys("wt", range(b + 1))
-        win = lambda b: T.w[:, C * b:C * b + 1920].indirect(oN)
-        for b in (3, 2): act(T.xn[:, b:4 * C:4], win(b), Act.Copy, xkeys(b), ["xn%d" % b], scale=1.0 / 64)
-        for b in (1, 0): ts(T.xn[:, b:4 * C:4], win(b), 1.0 / 64, None, Alu.mult, r=xkeys(b), w=["xn%d" % b])
-        if rnd == 2: act(T.nlb[:], T.pw[:].indirect(oN), Act.Identity, ["pw", "val", "oN"], ["nlb"], bias=128.0)
+        gsum(1)
+        pick(R("ek"), R("bw", 0, 2 * C), R("c8"))
+        gsum(2)
+        gsum(3)
+        ts(oN(NZ, C), R("ek", 2 * NZ + 7, None, 8), 4.0, sH, Alu.mult, Alu.add)
+        ts(oN(0, NZ), R("ek", 7, 2 * NZ, 8), 4.0, sN, Alu.mult, Alu.add)
+        act(R("xn", 4 * NZ, 4 * C), ind(R("w", 4 * K), oN(NZ, C)), Act.Copy, scale=1.0 / 64)
+        g1, g2 = (G1, G2) if rnd < 2 else (G3, G4)
+        act(R("xn", 0, 4 * g1), ind(R("w"), oN(0, g1)), Act.Copy, scale=1.0 / 64)
+        if rnd == 2:
+            for i in range(2): pick(R("en", C * i, C * (i + 1)), R("bw", i, 2 * C, 2), R("c16"))
+            ts(H1, R("en", 15, C, 16), float(NZ), None, Alu.add)
+        ts(R("xn", 4 * g2, 4 * NZ), ind(R("w"), oN(g2, NZ)), 1.0 / 64, None, Alu.mult)
+        if rnd == 2: tt(H1, H1, R("en", C + 15, None, 16), Alu.max)
+        high(rnd + 1)
+        if rnd == 2: ts(oL, H1, BL + 128, None, Alu.add)
+        ts(R("xn", 4 * g1, 4 * g2), ind(R("w"), oN(g1, g2)), 1.0 / 64, None, Alu.mult)
 
-    h, o = C // 2, 3 * C
-    dma("S", T.oc[:], T.qx[:, o:o + C].bitcast(u8), qk)
-    mm("pD0", h, (T.qv[:], T.sv[:]), (T.qx[:, o:o + h], T.sx[:, o:o + h]), ["qv", qk[0]])
-    mm("pD1", h, (T.qv[:], T.sv[:]), (T.qx[:, o + h:o + C], T.sx[:, o + h:o + C]), ["qv", qk[1]])
-    cp(T.yb[:, 0:h], T.pD0[:, 0:h], ["p_pD0"], ["ya"])
-    cp(T.yb[:, h:C], T.pD1[:, 0:h], ["p_pD1"], ["yb"])
-    dma("A", T.nl[:], T.nlb[0:128:16, :], ["nlb"])
-    dma("S", T.y[:, 0:h], T.yb[:, 0:h], ["ya"])
-    dma("A", T.y[:, h:C], T.yb[:, h:C], ["yb"])
-    for k in range(4): dma("S" if k < 2 else "A", T.osc[4 * k:4 * k + 4, :], T.sx[32 * k:32 * k + 4, o:o + C], qk)
+    o = 3 * CP
+    QV = Q("v")
+    mm("pD0", QV, Q("x", o + NZ, o + CP))
+    dma("S", T.oc[:, 4 * NZ:4 * C], raw(R("qx", o + NZ, o + C)))
+    pack(3, 128, NZ)
+    pack(3, 0, 128)
+    act(R("nlb"), ind(R("nw"), oL), Act.Identity, bias=128.0)
+    mm("pD1", QV, Q("x", o + 128, o + NZ))
+    mm("pD2", QV, Q("x", o, o + 128))
+    cp(R("yb", NZ, C), R("pD0", 0, A2))
+    dma("S", T.oc[:, 0:4 * NZ], raw(R("qx", o, o + NZ)))
+    dma("S", T.y[:, NZ:C], R("yb", NZ, C))
+    cp(R("yb", 128, NZ), R("pD1", 0, NZ - 128))
+    cp(R("yb", 0, 128), R("pD2", 0, 128))
+    add("A", lambda: g.scalar.dma_start(T.nl[:], T.nlb[0:128:16, :]), [R("nlb")], kind="dma")
+    dma("S", T.y[:, 128:NZ], R("yb", 128, NZ))
+    dma("A", T.y[:, 0:128], R("yb", 0, 128))
+    for k in range(4):
+        add("SA"[k % 2], lambda k=k: queue["SA"[k % 2]].dma_start(T.osc[4 * k:4 * k + 4, :], T.sx[32 * k:32 * k + 4, o:o + C]), [R("sx", o, o + C)], kind="dma")
 
     needed = set()
     for op in ops: needed.update(op["deps"])

@@ -9,11 +9,11 @@ BIG = 2.0 ** 90
 B = 4096.0
 BL = 1792.0
 MARK = -512.0
-TILES = [["d", 0, 1, 2], [3, 4, 5, 6], [7, 8, 9, 10], [11, 12, 13, 14], [15, 16, 17, 18], [19, 20, 21, 22]]
+TILES = [["d", 23, 22, 21], [20, 19, 18, 17], [16, 15, 14, 13], [12, 11, 10, 9], [8, 7, 6, 5], [4, 3, 2, 1]]
 TN = [384, 320, 256, 192, 128, 128]
-VK = 6
-MID = 96
-G1, G2, G3, G4 = 128, 200, 128, 200
+VS, VLO, VHI = 1, 15, 21
+ZA = 128
+G1, G2, G3 = 128, 224, 128
 
 F8, U8, BF, F32, F16 = "float8_e4m3fn_x4", "uint8", "bfloat16", "float32", "float16"
 SCRATCH = {"ci": ("sbuf", [128, 16], "int32"), "offu": ("sbuf", [128, 8], "uint16"), "off": ("sbuf", [128, 240], "uint16")}
@@ -21,11 +21,11 @@ for _n, _w in [("u", 128), ("u2", 128), ("v", 128), ("w", 512), ("x", 4 * CP), (
     SCRATCH["q" + _n] = ("sbuf", [128, _w], F8)
     SCRATCH["s" + _n] = ("sbuf", [128, _w], U8)
 for _n, _w in [("x0", 4 * CP), ("xn", 4 * CP), ("ut", 512), ("vt", 512), ("ones", 516), ("eb", 516), ("go", 512),
-               ("tt", NZ), ("cm0", NZ), ("cmax", NZ), ("chold", NZ), ("cx", 256), ("c8", 2 * C), ("c16", C), ("keep", NZ), ("sig", NZ * (23 - VK)), ("ds", C),
+               ("tt", 256), ("cm0", 144), ("cmin", 144), ("chold", 144), ("cx", 256), ("c8", 2 * C), ("c32", 2 * C), ("keep", 192), ("sig", 8 * 23 * 24), ("ds", C),
                ("ad", 192), ("adp", 192), ("ha", 400), ("hb", 400), ("pw", 1440), ("nw", NZ + C), ("bw", 2320), ("ur", C), ("w", 4 * (NZ + C)), ("tp", 4 * C),
-               ("zf", 4 * C), ("z", 4 * K), ("jb", 192 * VK)]:
+               ("zf", 4 * C), ("z", 4 * K), ("jb", 192 * (VHI + 1 - VLO))]:
     SCRATCH[_n] = ("sbuf", [128, _w], BF)
-for _n, _w in [("cf", 256), ("d1", C), ("pb", C), ("jv", 24), ("csx", C), ("sa", 256), ("sb", 512), ("nlb", C), ("yb", C)]:
+for _n, _w in [("cf", 256), ("d1", C), ("pb", C), ("jv", C), ("csx", C), ("sa", 256), ("sb", 512), ("nlb", C), ("yb", C)]:
     SCRATCH[_n] = ("sbuf", [128, _w], F32)
 for _n, _w in [("ex", NZ), ("ek", 2 * C), ("en", 2 * C)]:
     SCRATCH[_n] = ("sbuf", [128, _w], F16)
@@ -117,51 +117,59 @@ def rank_program(g, core, T, topo):
     iota(ci(0, 1), [[0, 1]], 0, 1)
     fill(R("ones"), 1.0)
     iota(K16, [[16, 24]], 0, 0)
-    iota(R("tt"), [[0, 17], [1, 16]], 0, 0)
+    iota(R("tt"), [[0, 16], [1, 16]], 0, 0)
     add("G", lambda: g.affine_select(T.eb[:], T.ones[:], [[-1, 516]], Alu.is_equal, 0.0, 3, 4), [R("ones")], [R("eb")])
     ts(ci(1, 2), ci(0, 1), 15, None, Alu.bitwise_and)
     ts(ci(2, 3), ci(0, 1), 0x70, None, Alu.bitwise_and)
     ts(ci(3, 4), ci(0, 1), 2, 3, Alu.arith_shift_right, Alu.bitwise_and)
     ts(ci(4, 5), ci(0, 1), 3, None, Alu.bitwise_and)
+    tail = lambda m: fill(R("bt%d" % m, 64 * TILES[m][3] if m < 5 else 0), 0.0)
     fill(R("x0", 4 * C), 0.0)
-    cp(R("cf", 0, 4), ci(1, 5))
     cp(R("offu"), R("cf", 16, 24))
-    fill(R("bt5"), 0.0)
+    for m in (0, 1): tail(m)
+    cp(R("cf", 0, 4), ci(1, 5))
+    tail(5)
     ts(R("cf", 200, 208), R("cf", 16, 24), gq, None, Alu.is_equal)
-    ts(qa, qc, 0.5, None, Alu.add)
-    qz((R("qb3", 128), R("sc3", 128)), R("bt5"))
-    act(qr, qc, Act.Identity, scale=2 * B, bias=-29 * B)
-    act(qd, qc, Act.Square, bias=1.0)
+    ts(qa, qc, -0.5, None, Alu.add)
+    ts(R("cm0"), R("tt", 0, 144), qc, 0.5, Alu.is_equal, Alu.subtract)
+    for m in (2, 3): tail(m)
+    ts(R("chold"), R("tt", 0, 144), qa, -2 * BIG, Alu.subtract, Alu.mult)
+    tail(4)
+    act(qr, qc, Act.Identity, scale=-2 * B, bias=B)
+    act(qd, qc, Act.Square, bias=-16.0)
     act(J, K16, Act.Identity, bias=qc)
+    act(R("keep"), R("tt", 0, 192), Act.Sign)
+    act(R("cmin"), R("cm0"), Act.Copy, scale=2 * BIG)
     for j in range(8): act(R("go", 64 * j, 64 * j + 64), R("ones", 0, 64), Act.Copy, scale=R("cf", 200 + j, 201 + j))
-    for m in range(5): fill(R("bt%d" % m, 4 * (368 - 16 * TILES[m][3])), 0.0)
-    ts(R("cm0"), R("tt"), qc, 0.5, Alu.is_equal, Alu.subtract)
-    ts(R("chold"), R("tt"), qa, -2 * BIG, Alu.subtract, Alu.mult)
-    act(qd, qd, Act.Identity, scale=-B, bias=-B)
-    act(KA, J, Act.Identity, bias=-NZ - B)
-    act(R("cmax"), R("cm0"), Act.Copy, scale=-2 * BIG)
-    act(R("keep"), R("tt"), Act.Sign)
-    act(R("cx"), R("tt", 0, 256), Act.Identity, scale=2 * B, bias=qr)
-    act(R("cf", 64, 64 + VK), R("cf", 64, 64 + VK), Act.Identity, bias=128.0)
-    act(R("cx", 15, 256, 16), R("cx", 15, 256, 16), Act.Identity, bias=qd)
-    for z in (R("jv", 23), R("ad"), R("ha", 128, 144), R("hb", 128, 144), R("xn", 4 * C)): iota(z, [[0, len(z[1])]], 0, 0)
+    for z in (R("jv", 15, 16), R("ad"), R("ha", 128, 144), R("hb", 128, 144), R("xn", 4 * C)): iota(z, [[0, len(z[1])]], 0, 0)
     E = lambda b: Q("e", 128 * b, 128 * (b + 1))
-    qz(Q("g"), R("go"))
-    ts(R("c8", 0, None, 2), R("ones", 0, C), float(NZ), None, Alu.mult)
-    qz(E(0), R("eb", 3, 515))
     qz(Q("u"), R("ut"))
     act(R("su2"), ind(R("su"), R("offu")), Act.Copy)
+    for a, b in ((NZ, CP), (0, 128)): qz(Q("x", a, b), R("x0", 4 * a, 4 * b))
     cp(words(R("qu2")), ind(words(R("qu")), R("offu")))
+    qz(Q("x", 128, NZ), R("x0", 512, 4 * NZ))
+    mm("pD0", Q("u2"), Q("x", NZ, CP))
+    qz((R("qb3", 128), R("sc3", 128)), R("bt5"))
+    qz(Q("g"), R("go"))
+    ts(R("c8", 0, None, 2), R("ones", 0, C), float(NZ), None, Alu.mult)
+    act(qd, qd, Act.Identity, scale=-B, bias=-B)
+    act(KA, J, Act.Identity, scale=-1.0, bias=NZ - B)
+    act(R("cx"), R("tt"), Act.Identity, scale=2 * B, bias=qr)
+    act(R("cf", 64 + VLO, 65 + VHI), R("cf", 64 + VLO, 65 + VHI), Act.Identity, bias=128.0)
     act(sH, r4, Act.Identity, scale=-2 * BL, bias=BL)
     act(e4, r4, Act.Square, bias=-4.0)
     act(sF, b4, Act.Identity, bias=4 * (BL + 128))
     act(R("cf", 208, 212), R("tt", 0, 4), Act.Identity, scale=2 * BL, bias=sH)
     act(e4, e4, Act.Identity, scale=-BL, bias=-BL)
     act(sN, r4, Act.Identity, scale=4.0 * NZ, bias=sF)
-    act(R("cf", 211, 212), R("cf", 211, 212), Act.Identity, bias=e4)
-    act(sN, sN, Act.Identity, bias=-12.0 * NZ)
-    for t in range(4): act(R("c8", 2 * t + 1, None, 8), R("ones", 0, 96), Act.Copy, scale=R("cf", 208 + t, 209 + t))
-    act(sH, sN, Act.Identity, bias=-4.0 * K)
+    act(R("cx", 15, 256, 16), R("cx", 15, 256, 16), Act.Identity, bias=qd)
+    def lists():
+        act(R("cf", 211, 212), R("cf", 211, 212), Act.Identity, bias=e4)
+        act(sN, sN, Act.Identity, bias=-12.0 * NZ)
+        act(J2, J, Act.Identity, bias=float(NZ), scale=2.0)
+        act(TR2, J, Act.Identity, bias=float(C - 1))
+        for t in range(4): act(R("c8", 2 * t + 1, None, 8), R("ones", 0, 96), Act.Copy, scale=R("cf", 208 + t, 209 + t))
+        act(sH, sN, Act.Identity, bias=-4.0 * K)
     U2 = Q("u2")
 
     place = {}
@@ -170,26 +178,14 @@ def rank_program(g, core, T, topo):
     def plane(k, a, b):
         m, t = place[k]
         return R("bt%d" % m, 4 * a + t, 4 * b, 4)
-    def back(k, a, b):
-        m, t = place[k]
-        return R("bt%d" % m, 4 * (C - 1 - a) + t, 4 * (C - 1 - b) + t if b < C else None, -4)
-    piv = lambda k: R("pb", 16 * k + 15, 16 * k + 16)
+    piv = lambda k: R("pb", 16 * k, 16 * k + 1)
     second = ["pV", "pA", "pC1", "pC0"]
-    sig = lambda k: R("sig", NZ * (k - VK), NZ * (k - VK) + 368 - 16 * k)
-    def relu(k): act(back(k, 16 * k + 16, C), sig(k), Act.Relu, scale=-1.0, accum_out=R("jv", k, k + 1))
-    def sign(k): act(sig(k), R("pD1", 16 * k + 16 - NZ, A2) if 16 * k >= NZ else R("pA", 16 * k + 16, C), Act.Sign, bias=piv(k), scale=-1.0)
-    def signs(ks, lag):
-        for i in range(len(ks) + lag):
-            if i < len(ks): sign(ks[i])
-            if i >= lag: relu(ks[i - lag])
-    def hold(lo, hi, src, between=None):
-        tt(R("d1", lo, hi), src, R("cmax", 0, hi - lo), Alu.max)
-        if between: between()
-        scan(R("pb", lo, hi), R("chold", 0, hi - lo), R("d1", lo, hi), 0.0, Alu.max, Alu.min)
-    def within(lo, hi, src, between=None):
-        tt(back("d", lo, hi), src, R("pb", lo, hi), Alu.is_gt)
-        if between: between()
-        scan(R("ds", C - hi, C - lo), R("keep", 0, hi - lo), plane("d", C - hi, C - lo), 0.0, Alu.mult, Alu.add)
+    sig = lambda k: R("sig", 8 * k * (k - 1), 8 * k * (k + 1))
+    def relu(k): act(plane(k, 0, 16 * k), sig(k), Act.Relu, accum_out=R("jv", 16 * k + 15, 16 * k + 16))
+    def sign(k): act(sig(k), R("pA", 0, 16 * k), Act.Sign, bias=piv(k), scale=-1.0)
+    def back(n, lo, hi): return R(n, hi - 1, lo - 1 if lo else None, -1)
+    def own(lo, hi, src): tt(R("d1", lo, hi), src, R("cmin", 0, hi - lo), Alu.min)
+    def hold(lo, hi): scan(back("pb", lo, hi), back("chold", 0, hi - lo), back("d1", lo, hi), 0.0, Alu.min, Alu.max)
 
     def blocks(src, h, fill1, fill2):
         tr(R(h, 64, 128), src)
@@ -211,91 +207,95 @@ def rank_program(g, core, T, topo):
     def pack(rnd, a, b): qz(Q("x", CP * rnd + a, CP * rnd + b), R(state(rnd), 4 * a, 4 * b))
     def high(rnd):
         pack(rnd, NZ, CP)
-        if rnd < 3:
-            for bank in ("pD0", "pD1"): mm(bank, U2, Q("x", CP * rnd + NZ, CP * (rnd + 1)))
+        if rnd < 3: mm("pD0", U2, Q("x", CP * rnd + NZ, CP * (rnd + 1)))
 
-    high(0)
-    qz(E(1), R("eb", 2, 514))
     for rnd in range(3):
         QX, QL = Q("x", CP * rnd, CP * rnd + C), Q("xl", C * rnd, C * (rnd + 1))
         dst = T.cores[rank ^ STEP[rnd]]
         ne = len(topo.engines(dst, core))
-        hold(NZ, C, R("pD0", 0, A2), lambda: pack(rnd, 128, NZ))
-        pack(rnd, 0, 128)
-        for bank in ("pV", "pA"): mm(bank, U2, QX)
+        own(NZ, C, R("pD0", 0, A2))
+        if rnd == 0: qz(E(0), R("eb", 3, 515))
+        else:
+            pack(rnd, 0, 128)
+            pack(rnd, 128, NZ)
+        hold(NZ, C)
+        for bank in ("pA", "pV"): mm(bank, U2, QX)
         send(dst, raw(QL[0]), raw(QX[0]), "ax%d" % rnd)
         send(dst, QL[1], QX[1], "ax%d" % rnd)
         add("-", None, w=QL, kind="ext", tok=("ax%d" % rnd, 2 * ne))
         add("-", None, w=[R("adp", 64 * rnd, 64 * rnd + 64)], kind="ext", tok=("af%d" % rnd, ne))
-        signs(list(range(22, 16, -1)), 5)
         if rnd == 0:
             iota(val, [[1, C]], -128, 0)
             add("S", lambda: g.sync.dma_start(T.qw[:].bitcast(u8), T.wc[:]), QL, [R("qw")], kind="dma")
             dma("S", R("vt"), T.v[:])
             dma("S", R("sw"), T.ws[:])
-        within(NZ, C, R("pD0", 0, A2))
-        hold(MID, NZ, R("pV", MID, NZ), lambda: tt(R("d1", 0, MID), R("pV", 0, MID), R("cmax", 0, MID), Alu.max))
-        scan(R("pb", 0, MID), R("chold", 0, MID), R("d1", 0, MID), 0.0, Alu.max, Alu.min)
-        signs(list(range(VK, 17)), 2)
         G = Q("g")
         def tile(m):
             q = lambda a, b: (R("qb%d" % m, a, b), R("sc%d" % m, a, b))
             qz(q(0, TN[m]), R("bt%d" % m, 0, 4 * TN[m]))
-            mm("pC0", G, q(0, 128), m == 5, m == 4)
+            mm("pC0", G, q(0, 128), m == 0, m == 5)
             if m < 4: mm("pC1", G, q(128, max(256, TN[m])), m == 0, m == 3)
-        def compare(k): ts(back(k, 16 * k + 16, C), R("pV", 16 * k + 16, C), piv(k), None, Alu.is_gt)
+        def compare(k): ts(plane(k, 0, 16 * k), R("pV", 0, 16 * k), piv(k), None, Alu.is_lt)
         def rows(k):
-            n = 184 - 8 * k
-            scan(R("jb", 192 * k + 192 - n, 192 * k + 192), plane(k, 0, n), plane(k, n, 2 * n), -128.0, Alu.add, Alu.add)
-        within(0, NZ, R("pV", 0, NZ), lambda: tile(5))
-        for k in range(3): compare(k)
-        rows(0)
+            e = 192 * (k - VLO + 1)
+            scan(R("jb", e - 8 * k, e), plane(k, 0, 8 * k), plane(k, 8 * k, 16 * k), -128.0, Alu.add, Alu.add)
+        if rnd > 0:
+            for b in (1, 2, 3, 0): mm("pD%d" % b, E(b), QX)
+        own(128, NZ, R("pV", 128, NZ))
+        own(0, 128, R("pV", 0, 128))
+        compare(VHI)
+        hold(128, NZ)
+        hold(0, 128)
+        for k in range(23, VHI, -1): sign(k)
+        for k in range(23, VHI, -1): relu(k)
+        ks = list(range(VLO - 1, VS, -1))
+        for i in range(len(ks) + 4):
+            if i < len(ks): sign(ks[i])
+            if i >= 4: relu(ks[i - 4])
+        compare(VHI - 1)
+        tt(plane("d", 0, C), R("pV", 0, C), R("pb"), Alu.is_lt)
+        for k in range(VHI - 2, 16, -1): compare(k)
         tile(0)
-        for k in range(3, VK): compare(k)
-        tt(KD, R("ds", C - 1, None, -16), KA, Alu.add)
-        def theirs(*bs):
-            for b in bs:
-                if rnd > 0: mm("pD%d" % b, E(b), QL)
-        rows(1)
-        rows(2)
+        for k in range(16, VLO - 1, -1): compare(k)
         tile(1)
-        theirs(0)
-        for k in range(3, VK): rows(k)
+        for a in (0, 192): scan(R("ds", a, a + 192), R("keep", 0, 192), plane("d", a, a + 192), 0.0, Alu.mult, Alu.add)
         tile(2)
-        theirs(1)
+        for k in range(VHI, VLO + 1, -1): rows(k)
+        for k in range(1, VS + 1): compare(k)
         tile(3)
+        tt(KD, R("ds", 15, None, 16), KA, Alu.add)
+        for k in range(1, VS + 1): scan(R("jv", 16 * k + 16 - 8 * k, 16 * k + 16), plane(k, 0, 8 * k), plane(k, 8 * k, 16 * k), 0.0, Alu.add, Alu.add)
         tile(4)
-        theirs(2, 3)
-        tt(R("sa", 24, 24 + VK), R("sa", 0, VK), R("jb", 191, None, 192), Alu.add)
-        tt(R("sa", 24 + VK, 48), R("sa", VK, 24), R("jv", VK, 24), Alu.add)
-        fill(R("bw", 0, 2 * C), MARK)
+        for k in range(VLO + 1, VLO - 1, -1): rows(k)
+        tile(5)
+        if rnd == 0:
+            lists()
+            for b in (1, 2, 3): qz(E(b), R("eb", 3 - b, 515 - b))
+            for b in range(4): mm("pD%d" % b, E(b), QX)
+        for b in range(4): act(R("w", 4 * NZ + b, None, 4), R("pD%d" % b, 0, C), Act.Copy, scale=64.0)
+        for a, b in ((0, VLO), (VHI + 1, 24)): tt(R("sa", 24 + a, 24 + b), R("sa", a, b), R("jv", 16 * a + 15, 16 * b, 16), Alu.add)
+        tt(R("sa", 24 + VLO, 25 + VHI), R("sa", VLO, VHI + 1), R("jb", 191, None, 192), Alu.add)
         pick(R("csx", 128, C), R("pC1", 0, 256), R("cx"))
+        ts(RD, RA, -float(K), None, Alu.add)
         pick(R("csx", 0, 128), R("pC0", 0, 128), R("cx", 0, 128))
-        ts(RD, RA, float(K), None, Alu.add)
+        fill(R("bw", 0, C), MARK)
         o = 64 * rnd
         AD, af, df = R("ad", o, o + 64), R("ad", o, o + 24), R("ad", o + 32, o + 56)
-        tt(af, R("csx", C - 1, None, -16), RA, Alu.is_gt)
-        tt(df, R("csx", C - 1, None, -16), RD, Alu.is_gt)
+        tt(af, R("csx", 15, None, 16), RA, Alu.is_lt)
+        tt(df, R("csx", 15, None, 16), RD, Alu.is_lt)
         send(dst, R("adp", o, o + 64), AD, "af%d" % rnd)
-        if rnd == 0:
-            for b in (2, 3): qz(E(b), R("eb", 3 - b, 515 - b))
-            act(J2, J, Act.Identity, bias=float(NZ), scale=2.0)
-            act(TR2, J, Act.Identity, bias=float(C - 1))
-            for b in range(4): mm("pD%d" % b, E(b), QL)
-        for b in range(4): act(R("tp", b, None, 4), R("pD%d" % b, 0, C), Act.Copy, scale=-1.0)
-        for b in range(4): mm(second[b], E(b), QX)
+        fill(R("bw", C, 2 * C), MARK)
+        for b in range(4): mm(second[b], E(b), QL)
+        for b in range(4): act(R("tp", b, None, 4), R(second[b], 0, C), Act.Copy, scale=-1.0)
         for b in range(4): mm("pD%d" % b, E(b), QX, True, False)
-        for b in range(4): act(R("w", 4 * NZ + b, None, 4), R(second[b], 0, C), Act.Copy, scale=64.0)
         def spare():
             if rnd == 1:
                 qz(Q("v"), R("vt"))
                 ts(q17, qc, -17.0, BL, Alu.add, Alu.mult)
-            if rnd == 2: ts(R("c16"), R("c16"), 2 * BL, None, Alu.mult)
+            if rnd == 2: ts(R("c32", 1, None, 2), R("c32", 1, None, 2), 2 * BL, None, Alu.mult)
         blocks(AD, "ha", lambda: ts(R("sa", 192, 256), AD, -4096.0, 4094.0, Alu.mult, Alu.add), spare)
-        qz(Q("t"), R("tp"))
-        for b in range(4): mm("pD%d" % b, E(b), Q("t"), False, True)
         def diff(b): act(R("zf", b, None, 4), R("pD%d" % b, 0, C), Act.Copy)
-        for b in range(3): diff(b)
+        def theirs(a, b): qz(Q("t", a, b), R("tp", 4 * a, 4 * b))
         upto(CA, "ha", 0, 0.0)
         upto(CD, "ha", 1, 0.0)
         tt(T2, R("sa", 224, 248), TR2, Alu.min)
@@ -308,56 +308,60 @@ def rank_program(g, core, T, topo):
             tt(N2, J2, T1, Alu.min)
             tt(CF, CF, T2, Alu.add)
             ts(HB, m2, -4096.0, 4096.0, Alu.mult, Alu.add)
-        blocks(R("hb", 0, 64), "hb", fill1, lambda: tt(N3, N2, U1, Alu.add))
-        if rnd == 1:
-            for a in (0, 192): ts(R("c16", a, a + 192), R("tt", 0, 192), qc, 0.5, Alu.is_ge, Alu.subtract)
-        if rnd == 2: ts(R("c16", 15, None, 16), R("c16", 15, None, 16), q17, None, Alu.add)
+        def fill2():
+            tt(N3, N2, U1, Alu.add)
+            theirs(0, 192)
+        blocks(R("hb", 0, 64), "hb", fill1, fill2)
+        theirs(192, C)
+        for b in range(4): mm("pD%d" % b, E(b), Q("t"), False, True)
         scan(R("sb", 287, 263, -1), R("hb", 296, 272, -1), R("hb", 359, 335, -1), 1.0, Alu.add, Alu.add)
-        upto(CS, "hb", 0, -1.0)
         upto(C2, "hb", 1, 0.0)
+        upto(CS, "hb", 0, -1.0)
+        act(R("sb", 320, 448), R("hb", 272, 400), Act.Copy, accum_out=TOT)
+        act(CT, CF, Act.Identity, bias=TOT)
+        for b in range(4): diff(b)
         tt(POS, N3, SF, Alu.add)
         tt(CM, CS, C2, Alu.add)
         tt(POS, POS, CS, Alu.max)
-        tt(X1, CF, CM, Alu.subtract)
         tt(H, CM, HB, Alu.add)
+        tt(X1, CT, CM, Alu.subtract)
         cp(oP, POS)
-        act(R("sb", 320, 448), R("hb", 272, 400), Act.Copy, accum_out=TOT)
-        diff(3)
-        act(CT, X1, Act.Identity, bias=TOT)
+        tt(H, H, X1, Alu.min)
         cp(ind(R("pw"), oP), val)
-        tt(H, H, CT, Alu.min)
-        pick(R("ex"), R("pw", 0, NZ), R("c8", 1, 2 * NZ, 2))
         ts(oB, H, 2.0, None, Alu.mult)
+        pick(R("ex"), R("pw", 0, NZ), R("c8", 1, 2 * NZ, 2))
+        for a in (0, C):
+            if rnd == 0: ts(R("c32", a, a + C, 2), R("tt", 0, 192), qc, float(NZ), Alu.is_equal, Alu.mult)
+            if rnd == 1: ts(R("c32", a + 1, a + C, 2), R("tt", 0, 192), qc, 0.5, Alu.is_ge, Alu.subtract)
+        if rnd == 2: ts(R("c32", 31, None, 32), R("c32", 31, None, 32), q17, None, Alu.add)
         ts(oF(0, NZ), R("ex", 3, None, 4), 4.0, sF, Alu.mult, Alu.add)
-        if rnd == 2: act(R("nw", 0, NZ), R("pw", 0, NZ), Act.Copy)
         T64 = R("w", 4 * NZ)
-        act(R("z"), ind(R("zf"), oF(0, K)), Act.Copy)
+        act(R("z", 0, 4 * ZA), ind(R("zf"), oF(0, ZA)), Act.Copy)
         cp(ind(R("bw"), oB), val)
-        qz(Q("z"), R("z"))
+        cp(R("z", 4 * ZA), ind(R("zf"), oF(ZA, K)))
         act(R("w", 0, 4 * K), ind(T64, oF(0, K)), Act.Copy)
         act(R("w", 4 * K, 4 * NZ), ind(T64, oF(K, NZ)), Act.Copy)
-        for b in range(4): mm(second[b], Q("w", 128 * b, 128 * (b + 1)), Q("z"))
+        if rnd == 2: act(R("nw", 0, NZ), R("pw", 0, NZ), Act.Copy)
         def gsum(b): tt(R("w", b, 4 * K, 4), R(second[b], 0, K), R("w", b, 4 * K, 4), Alu.add)
         ts(R("ur"), R("bw", 0, 2 * C, 2), MARK, None, Alu.is_equal)
+        qz(Q("z"), R("z"))
+        for b in range(4): mm(second[b], Q("w", 128 * b, 128 * (b + 1)), Q("z"))
         scan(R("bw", 1, 2 * C, 2), R("ones", 0, C), R("ur"), -129.0, Alu.mult, Alu.add)
-        gsum(0)
-        gsum(1)
-        pick(R("ek"), R("bw", 0, 2 * C), R("c8"))
-        gsum(2)
-        gsum(3)
+        pick(R("ek", 2 * NZ), R("bw", 2 * NZ, 2 * C), R("c8", 0, 2 * A2))
+        pick(R("ek", 0, 2 * NZ), R("bw", 0, 2 * NZ), R("c8", 0, 2 * NZ))
         ts(oN(NZ, C), R("ek", 2 * NZ + 7, None, 8), 4.0, sH, Alu.mult, Alu.add)
+        for b in range(2): gsum(b)
         ts(oN(0, NZ), R("ek", 7, 2 * NZ, 8), 4.0, sN, Alu.mult, Alu.add)
+        for b in range(2, 4): gsum(b)
+        def new(a, b): ts(R("xn", 4 * a, 4 * b), ind(R("w"), oN(a, b)), 1.0 / 64, None, Alu.mult)
         act(R("xn", 4 * NZ, 4 * C), ind(R("w", 4 * K), oN(NZ, C)), Act.Copy, scale=1.0 / 64)
-        g1, g2 = (G1, G2) if rnd < 2 else (G3, G4)
+        g1 = G1 if rnd < 2 else G3
         act(R("xn", 0, 4 * g1), ind(R("w"), oN(0, g1)), Act.Copy, scale=1.0 / 64)
-        if rnd == 2:
-            for i in range(2): pick(R("en", C * i, C * (i + 1)), R("bw", i, 2 * C, 2), R("c16"))
-            ts(H1, R("en", 15, C, 16), float(NZ), None, Alu.add)
-        ts(R("xn", 4 * g2, 4 * NZ), ind(R("w"), oN(g2, NZ)), 1.0 / 64, None, Alu.mult)
-        if rnd == 2: tt(H1, H1, R("en", C + 15, None, 16), Alu.max)
+        if rnd == 2: pick(R("en"), R("bw", 0, 2 * C), R("c32"))
+        new(G2, NZ)
+        if rnd == 2: ts(oL, R("en", 31, None, 32), BL + 128, None, Alu.add)
         high(rnd + 1)
-        if rnd == 2: ts(oL, H1, BL + 128, None, Alu.add)
-        ts(R("xn", 4 * g1, 4 * g2), ind(R("w"), oN(g1, g2)), 1.0 / 64, None, Alu.mult)
+        new(g1, G2)
 
     o = 3 * CP
     QV = Q("v")

@@ -12,20 +12,24 @@ MARK = -512.0
 TILES = [["d", 23, 22, 21], [20, 19, 18, 17], [16, 15, 14, 13], [12, 11, 10, 9], [8, 7, 6, 5], [4, 3, 2, 1]]
 TN = [384, 320, 256, 192, 128, 128]
 VS, VLO, VHI = 1, 15, 21
+S1 = 4
+FA = 240
 ZA = 128
-G1, G2, G3 = 128, 224, 128
+L1, L2 = 200, 72
+G1, G2 = 128, 224
 
 F8, U8, BF, F32, F16 = "float8_e4m3fn_x4", "uint8", "bfloat16", "float32", "float16"
-SCRATCH = {"ci": ("sbuf", [128, 16], "int32"), "offu": ("sbuf", [128, 8], "uint16"), "off": ("sbuf", [128, 240], "uint16")}
+SCRATCH = {"ci": ("sbuf", [128, 16], "int32"), "fi": ("sbuf", [128, 96], "int32"), "fp": ("sbuf", [128, 96], "int32"),
+           "offu": ("sbuf", [128, 8], "uint16"), "off": ("sbuf", [128, 240], "uint16")}
 for _n, _w in [("u", 128), ("u2", 128), ("v", 128), ("w", 512), ("x", 4 * CP), ("xl", 3 * C), ("e", 512), ("g", 128), ("t", C), ("z", K)]:
     SCRATCH["q" + _n] = ("sbuf", [128, _w], F8)
     SCRATCH["s" + _n] = ("sbuf", [128, _w], U8)
 for _n, _w in [("x0", 4 * CP), ("xn", 4 * CP), ("ut", 512), ("vt", 512), ("ones", 516), ("eb", 516), ("go", 512),
-               ("tt", 256), ("cm0", 144), ("cmin", 144), ("chold", 144), ("cx", 256), ("c8", 2 * C), ("c32", 2 * C), ("keep", 192), ("sig", 8 * 23 * 24), ("ds", C),
-               ("ad", 192), ("adp", 192), ("ha", 400), ("hb", 400), ("pw", 1440), ("nw", NZ + C), ("bw", 2320), ("ur", C), ("w", 4 * (NZ + C)), ("tp", 4 * C),
+               ("tt", NZ), ("cm0", 144), ("cmin", 144), ("chold", 144), ("c8", 2 * C), ("c32", 2 * C), ("keep", NZ), ("sig", 8 * 23 * 24), ("ds", C),
+               ("ha", 400), ("hb", 400), ("pw", 1440), ("nw", NZ + C), ("bw", 2320), ("ur", C), ("w", 4 * (NZ + C)), ("tp", 4 * C),
                ("zf", 4 * C), ("z", 4 * K), ("jb", 192 * (VHI + 1 - VLO))]:
     SCRATCH[_n] = ("sbuf", [128, _w], BF)
-for _n, _w in [("cf", 256), ("d1", C), ("pb", C), ("jv", C), ("csx", C), ("sa", 256), ("sb", 512), ("nlb", C), ("yb", C)]:
+for _n, _w in [("cf", 256), ("cx", C), ("d1", C), ("pb", C), ("jv", C), ("csx", C), ("sa", 256), ("sb", 512), ("nlb", C), ("yb", C)]:
     SCRATCH[_n] = ("sbuf", [128, _w], F32)
 for _n, _w in [("ex", NZ), ("ek", 2 * C), ("en", 2 * C)]:
     SCRATCH[_n] = ("sbuf", [128, _w], F16)
@@ -103,21 +107,22 @@ def rank_program(g, core, T, topo):
         sent[0] += len(topo.engines(core, dst))
         add("G", lambda: g.remote_dma(o[2], a[2], T.sem[sem], T.sem.sent, pid, rid, topo.mask(core, dst)), [a], kind="remote")
     def iota(o, pat, base, cm):
-        kw = {} if o[0] == "ci" else {"allow_small_or_imprecise_dtypes": True}
+        kw = {} if o[0] in ("ci", "fi") else {"allow_small_or_imprecise_dtypes": True}
         add("G", lambda: g.iota(o[2], pat, base, cm, **kw), [], [o])
 
+    dma("S", R("ut", 0, 256), T.u[:, 0:256])
+    dma("A", R("ut", 256), T.u[:, 256:512])
     dma("S", R("x0", 4 * NZ, 4 * C), T.x[:, 4 * NZ:4 * C])
-    dma("A", R("ut"), T.u[:])
-    dma("S", R("x0", 512, 4 * NZ), T.x[:, 512:4 * NZ])
     dma("A", R("x0", 0, 512), T.x[:, 0:512])
+    dma("S", R("x0", 512, 4 * NZ), T.x[:, 512:4 * NZ])
     qc, gq, qa, qr, qd, ng, r4, b4, e4, sF, sN, sH, q17 = [R("cf", i, i + 1) for i in (0, 1, 4, 5, 6, 7, 2, 3, 8, 9, 10, 11, 12)]
-    K16, J, KA, J2, TR, TR2, J3 = [R("cf", 16 + 24 * i, 40 + 24 * i) for i in range(7)]
+    K16, J, KA, J2, TR2 = [R("cf", 16 + 24 * i, 40 + 24 * i) for i in range(5)]
     val = R("nw", NZ)
     ci = lambda a, b: R("ci", a, b)
     iota(ci(0, 1), [[0, 1]], 0, 1)
     fill(R("ones"), 1.0)
     iota(K16, [[16, 24]], 0, 0)
-    iota(R("tt"), [[0, 16], [1, 16]], 0, 0)
+    iota(R("tt"), [[0, 17], [1, 16]], 0, 0)
     add("G", lambda: g.affine_select(T.eb[:], T.ones[:], [[-1, 516]], Alu.is_equal, 0.0, 3, 4), [R("ones")], [R("eb")])
     ts(ci(1, 2), ci(0, 1), 15, None, Alu.bitwise_and)
     ts(ci(2, 3), ci(0, 1), 0x70, None, Alu.bitwise_and)
@@ -132,44 +137,40 @@ def rank_program(g, core, T, topo):
     ts(R("cf", 200, 208), R("cf", 16, 24), gq, None, Alu.is_equal)
     ts(qa, qc, -0.5, None, Alu.add)
     ts(R("cm0"), R("tt", 0, 144), qc, 0.5, Alu.is_equal, Alu.subtract)
-    for m in (2, 3): tail(m)
+    qz(Q("u"), R("ut"))
     ts(R("chold"), R("tt", 0, 144), qa, -2 * BIG, Alu.subtract, Alu.mult)
-    tail(4)
+    qz((R("qb3", 128), R("sc3", 128)), R("bt5"))
     act(qr, qc, Act.Identity, scale=-2 * B, bias=B)
+    act(ng, qc, Act.Identity, scale=-2 * B, bias=30 * B)
     act(qd, qc, Act.Square, bias=-16.0)
     act(J, K16, Act.Identity, bias=qc)
-    act(R("keep"), R("tt", 0, 192), Act.Sign)
+    act(R("keep"), R("tt"), Act.Sign)
     act(R("cmin"), R("cm0"), Act.Copy, scale=2 * BIG)
-    for j in range(8): act(R("go", 64 * j, 64 * j + 64), R("ones", 0, 64), Act.Copy, scale=R("cf", 200 + j, 201 + j))
-    for z in (R("jv", 15, 16), R("ad"), R("ha", 128, 144), R("hb", 128, 144), R("xn", 4 * C)): iota(z, [[0, len(z[1])]], 0, 0)
-    E = lambda b: Q("e", 128 * b, 128 * (b + 1))
-    qz(Q("u"), R("ut"))
     act(R("su2"), ind(R("su"), R("offu")), Act.Copy)
-    for a, b in ((NZ, CP), (0, 128)): qz(Q("x", a, b), R("x0", 4 * a, 4 * b))
+    for j in range(8): act(R("go", 64 * j, 64 * j + 64), R("ones", 0, 64), Act.Copy, scale=R("cf", 200 + j, 201 + j))
+    E = lambda b: Q("e", 128 * b, 128 * (b + 1))
     cp(words(R("qu2")), ind(words(R("qu")), R("offu")))
-    qz(Q("x", 128, NZ), R("x0", 512, 4 * NZ))
-    mm("pD0", Q("u2"), Q("x", NZ, CP))
-    qz((R("qb3", 128), R("sc3", 128)), R("bt5"))
-    qz(Q("g"), R("go"))
-    ts(R("c8", 0, None, 2), R("ones", 0, C), float(NZ), None, Alu.mult)
-    act(qd, qd, Act.Identity, scale=-B, bias=-B)
-    act(KA, J, Act.Identity, scale=-1.0, bias=NZ - B)
-    act(R("cx"), R("tt"), Act.Identity, scale=2 * B, bias=qr)
-    act(R("cf", 64 + VLO, 65 + VHI), R("cf", 64 + VLO, 65 + VHI), Act.Identity, bias=128.0)
+    for a, b in ((NZ, CP), (0, 128), (128, NZ)): qz(Q("x", a, b), R("x0", 4 * a, 4 * b))
+    for bank in ("pD0", "pD1"): mm(bank, Q("u2"), Q("x", NZ, CP))
+    for m in (2, 3, 4): tail(m)
+    act(qd, qd, Act.Identity, scale=-B, bias=ng)
+    for a in (0, 192): act(R("cx", a, a + 192), R("tt", 0, 192), Act.Identity, scale=2 * B, bias=qr)
+    act(KA, J, Act.Identity, bias=qd)
     act(sH, r4, Act.Identity, scale=-2 * BL, bias=BL)
     act(e4, r4, Act.Square, bias=-4.0)
     act(sF, b4, Act.Identity, bias=4 * (BL + 128))
-    act(R("cf", 208, 212), R("tt", 0, 4), Act.Identity, scale=2 * BL, bias=sH)
-    act(e4, e4, Act.Identity, scale=-BL, bias=-BL)
-    act(sN, r4, Act.Identity, scale=4.0 * NZ, bias=sF)
-    act(R("cx", 15, 256, 16), R("cx", 15, 256, 16), Act.Identity, bias=qd)
+    act(R("cf", 64 + VLO, 65 + VHI), R("cf", 64 + VLO, 65 + VHI), Act.Identity, bias=-128.0)
     def lists():
+        act(R("cf", 208, 212), R("tt", 0, 4), Act.Identity, scale=2 * BL, bias=sH)
+        act(e4, e4, Act.Identity, scale=-BL, bias=-BL)
+        act(sN, r4, Act.Identity, scale=4.0 * NZ, bias=sF)
+        act(J2, J, Act.Identity, bias=float(NZ), scale=2.0)
+        act(TR2, J, Act.Identity, bias=float(C + 1))
         act(R("cf", 211, 212), R("cf", 211, 212), Act.Identity, bias=e4)
         act(sN, sN, Act.Identity, bias=-12.0 * NZ)
-        act(J2, J, Act.Identity, bias=float(NZ), scale=2.0)
-        act(TR2, J, Act.Identity, bias=float(C - 1))
         for t in range(4): act(R("c8", 2 * t + 1, None, 8), R("ones", 0, 96), Act.Copy, scale=R("cf", 208 + t, 209 + t))
         act(sH, sN, Act.Identity, bias=-4.0 * K)
+        act(R("c8", 0, None, 2), R("ones", 0, C), Act.Copy, scale=float(NZ))
     U2 = Q("u2")
 
     place = {}
@@ -180,26 +181,25 @@ def rank_program(g, core, T, topo):
         return R("bt%d" % m, 4 * a + t, 4 * b, 4)
     piv = lambda k: R("pb", 16 * k, 16 * k + 1)
     second = ["pV", "pA", "pC1", "pC0"]
-    sig = lambda k: R("sig", 8 * k * (k - 1), 8 * k * (k + 1))
-    def relu(k): act(plane(k, 0, 16 * k), sig(k), Act.Relu, accum_out=R("jv", 16 * k + 15, 16 * k + 16))
-    def sign(k): act(sig(k), R("pA", 0, 16 * k), Act.Sign, bias=piv(k), scale=-1.0)
+    def relu(k): act(plane(k, 0, 16 * k), R("sig", 8 * k * (k - 1), 8 * k * (k + 1)), Act.Relu, accum_out=R("jv", 16 * k + 15, 16 * k + 16))
+    def sign(k, a, b, src): act(R("sig", 8 * k * (k - 1) + a, 8 * k * (k - 1) + b), src, Act.Sign, bias=piv(k), scale=-1.0)
     def back(n, lo, hi): return R(n, hi - 1, lo - 1 if lo else None, -1)
     def own(lo, hi, src): tt(R("d1", lo, hi), src, R("cmin", 0, hi - lo), Alu.min)
     def hold(lo, hi): scan(back("pb", lo, hi), back("chold", 0, hi - lo), back("d1", lo, hi), 0.0, Alu.min, Alu.max)
 
-    def blocks(src, h, fill1, fill2):
-        tr(R(h, 64, 128), src)
+    def blocks(h, fill1, fill2):
+        tr(R(h, 64, 128), R(h, 0, 64))
         fill1()
         scan(R(h, 144, 208), R("keep", 0, 64), R(h, 64, 128), 0.0, Alu.mult, Alu.add)
         scan(R(h, 271, 207, -1), R(h, 128, 64, -1), R("keep", 0, 64), 0.0, Alu.add, Alu.mult)
         fill2()
         tr(R(h, 272, 400), R(h, 144, 272))
     def upto(out, h, i, init): scan(out, R(h, 335 + 32 * i, 359 + 32 * i), R(h, 272 + 32 * i, 296 + 32 * i), init, Alu.add, Alu.add)
+    def behind(n, a, h, i, init): scan(back(n, a, a + 24), back(h, 273 + 32 * i, 297 + 32 * i), back(h, 336 + 32 * i, 360 + 32 * i), init, Alu.add, Alu.add)
 
-    KD, RA, RD, CA, CD, N2, CF, T1 = [R("sa", 24 * i, 24 * (i + 1)) for i in range(8)]
-    U1, N3, CS, POS, C2, CM, X1, HB, H, CT, H1, SF = [R("sb", 24 * i, 24 * (i + 1)) for i in range(12)]
-    T2 = R("sb", 448, 472)
-    TOT = R("sb", 300, 301)
+    KD, W1, T2, CA, N2, CF, T1 = [R("sa", 24 * i, 24 * (i + 1)) for i in range(7)]
+    U1, N3, CS, POS, CM, X1, HB, H = [R("sb", 24 * i, 24 * (i + 1)) for i in range(8)]
+    SM, SF = R("sb", 216, 240), R("sb", 264, 288)
     oP, oB, oL = R("off", 0, 24), R("off", 24, 48), R("off", 48, 72)
     oF = lambda a, b: R("off", 72 + a // 4, 72 + b // 4)
     oN = lambda a, b: R("off", 140 + a // 4, 140 + b // 4)
@@ -207,24 +207,40 @@ def rank_program(g, core, T, topo):
     def pack(rnd, a, b): qz(Q("x", CP * rnd + a, CP * rnd + b), R(state(rnd), 4 * a, 4 * b))
     def high(rnd):
         pack(rnd, NZ, CP)
-        if rnd < 3: mm("pD0", U2, Q("x", CP * rnd + NZ, CP * (rnd + 1)))
+        if rnd < 3:
+            for bank in ("pD0", "pD1"): mm(bank, U2, Q("x", CP * rnd + NZ, CP * (rnd + 1)))
 
     for rnd in range(3):
         QX, QL = Q("x", CP * rnd, CP * rnd + C), Q("xl", C * rnd, C * (rnd + 1))
         dst = T.cores[rank ^ STEP[rnd]]
         ne = len(topo.engines(dst, core))
         own(NZ, C, R("pD0", 0, A2))
-        if rnd == 0: qz(E(0), R("eb", 3, 515))
+        if rnd == 0:
+            qz(Q("g"), R("go"))
+            qz(E(1), R("eb", 2, 514))
         else:
             pack(rnd, 0, 128)
             pack(rnd, 128, NZ)
         hold(NZ, C)
-        for bank in ("pA", "pV"): mm(bank, U2, QX)
+        if rnd == 0: qz(E(0), R("eb", 3, 515))
+        if rnd == 1:
+            qz(Q("v"), R("vt"))
+            ts(q17, qc, -17.0, BL, Alu.add, Alu.mult)
+        if rnd == 2: ts(R("c32", 1, None, 2), R("c32", 1, None, 2), 2 * BL, None, Alu.mult)
+        for bank in ("pA", "pV"): mm(bank, U2, Q("x", CP * rnd, CP * rnd + NZ))
+        def compare(k, a, b, src): ts(plane(k, a, b), src, piv(k), None, Alu.is_lt)
+        def within(a, b, src): tt(plane("d", a, b), src, R("pb", a, b), Alu.is_lt)
+        def inblock(a, b): scan(R("ds", a, b), R("keep", 0, b - a), plane("d", a, b), 0.0, Alu.mult, Alu.add)
+        within(NZ, C, R("pD0", 0, A2))
+        for k in range(VHI, 17, -1): compare(k, NZ, 16 * k, R("pD0", 0, 16 * k - NZ))
+        inblock(NZ, C)
+        for k in range(23, VHI, -1): sign(k, NZ, 16 * k, R("pD1", 0, 16 * k - NZ))
         send(dst, raw(QL[0]), raw(QX[0]), "ax%d" % rnd)
         send(dst, QL[1], QX[1], "ax%d" % rnd)
         add("-", None, w=QL, kind="ext", tok=("ax%d" % rnd, 2 * ne))
-        add("-", None, w=[R("adp", 64 * rnd, 64 * rnd + 64)], kind="ext", tok=("af%d" % rnd, ne))
+        add("-", None, w=[R("fp", 32 * rnd, 32 * rnd + 32)], kind="ext", tok=("af%d" % rnd, ne))
         if rnd == 0:
+            for z in (R("jv", 15, 16), R("fi"), R("ha", 0, 144), R("hb", 0, 144), R("xn", 4 * C)): iota(z, [[0, len(z[1])]], 0, 0)
             iota(val, [[1, C]], -128, 0)
             add("S", lambda: g.sync.dma_start(T.qw[:].bitcast(u8), T.wc[:]), QL, [R("qw")], kind="dma")
             dma("S", R("vt"), T.v[:])
@@ -235,118 +251,142 @@ def rank_program(g, core, T, topo):
             qz(q(0, TN[m]), R("bt%d" % m, 0, 4 * TN[m]))
             mm("pC0", G, q(0, 128), m == 0, m == 5)
             if m < 4: mm("pC1", G, q(128, max(256, TN[m])), m == 0, m == 3)
-        def compare(k): ts(plane(k, 0, 16 * k), R("pV", 0, 16 * k), piv(k), None, Alu.is_lt)
+        def low(k): compare(k, 0, min(16 * k, NZ), R("pV", 0, min(16 * k, NZ)))
+        def lowsign(k): sign(k, 0, min(16 * k, NZ), R("pA", 0, min(16 * k, NZ)))
         def rows(k):
             e = 192 * (k - VLO + 1)
             scan(R("jb", e - 8 * k, e), plane(k, 0, 8 * k), plane(k, 8 * k, 16 * k), -128.0, Alu.add, Alu.add)
         if rnd > 0:
-            for b in (1, 2, 3, 0): mm("pD%d" % b, E(b), QX)
+            for b in (0, 1): mm("pD%d" % b, E(b), QX)
         own(128, NZ, R("pV", 128, NZ))
         own(0, 128, R("pV", 0, 128))
-        compare(VHI)
+        low(VHI)
         hold(128, NZ)
         hold(0, 128)
-        for k in range(23, VHI, -1): sign(k)
+        for k in range(23, VHI, -1): lowsign(k)
         for k in range(23, VHI, -1): relu(k)
         ks = list(range(VLO - 1, VS, -1))
         for i in range(len(ks) + 4):
-            if i < len(ks): sign(ks[i])
+            if i < len(ks): lowsign(ks[i])
             if i >= 4: relu(ks[i - 4])
-        compare(VHI - 1)
-        tt(plane("d", 0, C), R("pV", 0, C), R("pb"), Alu.is_lt)
-        for k in range(VHI - 2, 16, -1): compare(k)
+        low(VHI - 1)
+        within(0, NZ, R("pV", 0, NZ))
+        for k in range(VHI - 2, 16, -1): low(k)
         tile(0)
-        for k in range(16, VLO - 1, -1): compare(k)
+        for k in range(16, VLO - 1, -1): low(k)
         tile(1)
-        for a in (0, 192): scan(R("ds", a, a + 192), R("keep", 0, 192), plane("d", a, a + 192), 0.0, Alu.mult, Alu.add)
+        inblock(0, NZ)
         tile(2)
-        for k in range(VHI, VLO + 1, -1): rows(k)
-        for k in range(1, VS + 1): compare(k)
+        if rnd > 0:
+            for b in (2, 3): mm("pD%d" % b, E(b), QL)
+        for k in range(VHI, VHI - 3, -1): rows(k)
+        for k in range(1, VS + 1): low(k)
         tile(3)
-        tt(KD, R("ds", 15, None, 16), KA, Alu.add)
+        tt(KD, KA, R("ds", 15, None, 16), Alu.subtract)
+        for k in range(VHI - 3, VLO - 1, -1): rows(k)
         for k in range(1, VS + 1): scan(R("jv", 16 * k + 16 - 8 * k, 16 * k + 16), plane(k, 0, 8 * k), plane(k, 8 * k, 16 * k), 0.0, Alu.add, Alu.add)
+        def less(a, b, sums): tt(R("cx", 16 * a + 15, 16 * b, 16), R("sa", a, b), sums, Alu.subtract)
+        less(VHI + 1, 24, R("jv", 16 * VHI + 31, C, 16))
         tile(4)
-        for k in range(VLO + 1, VLO - 1, -1): rows(k)
+        less(8, VLO, R("jv", 143, 16 * VLO, 16))
+        less(VLO, VHI + 1, R("jb", 191, None, 192))
         tile(5)
-        if rnd == 0:
-            lists()
-            for b in (1, 2, 3): qz(E(b), R("eb", 3 - b, 515 - b))
-            for b in range(4): mm("pD%d" % b, E(b), QX)
-        for b in range(4): act(R("w", 4 * NZ + b, None, 4), R("pD%d" % b, 0, C), Act.Copy, scale=64.0)
-        for a, b in ((0, VLO), (VHI + 1, 24)): tt(R("sa", 24 + a, 24 + b), R("sa", a, b), R("jv", 16 * a + 15, 16 * b, 16), Alu.add)
-        tt(R("sa", 24 + VLO, 25 + VHI), R("sa", VLO, VHI + 1), R("jb", 191, None, 192), Alu.add)
-        pick(R("csx", 128, C), R("pC1", 0, 256), R("cx"))
-        ts(RD, RA, -float(K), None, Alu.add)
+        def mine(b, bank): act(R("w", 4 * NZ + b, None, 4), R(bank, 0, C), Act.Copy, scale=64.0)
+        def minus(b, bank): act(R("tp", b, None, 4), R(bank, 0, C), Act.Copy, scale=-1.0)
+        if rnd == 0: lists()
+        else:
+            for b in (2, 3): minus(b, "pD%d" % b)
+        for b, bank in ((0, "pA"), (1, "pV")):
+            mm(bank, E(b), QL)
+            minus(b, bank)
+        less(0, 8, R("jv", 15, 128, 16))
+        pick(R("csx", 128, C), R("pC1", 0, 256), R("cx", 128, C))
+        if rnd == 0: qz(E(2), R("eb", 1, 513))
+        else: fill(R("bw", 0, C), MARK)
         pick(R("csx", 0, 128), R("pC0", 0, 128), R("cx", 0, 128))
-        fill(R("bw", 0, C), MARK)
-        o = 64 * rnd
-        AD, af, df = R("ad", o, o + 64), R("ad", o, o + 24), R("ad", o + 32, o + 56)
-        tt(af, R("csx", 15, None, 16), RA, Alu.is_lt)
-        tt(df, R("csx", 15, None, 16), RD, Alu.is_lt)
-        send(dst, R("adp", o, o + 64), AD, "af%d" % rnd)
-        fill(R("bw", C, 2 * C), MARK)
-        for b in range(4): mm(second[b], E(b), QL)
-        for b in range(4): act(R("tp", b, None, 4), R(second[b], 0, C), Act.Copy, scale=-1.0)
-        for b in range(4): mm("pD%d" % b, E(b), QX, True, False)
-        def spare():
-            if rnd == 1:
-                qz(Q("v"), R("vt"))
-                ts(q17, qc, -17.0, BL, Alu.add, Alu.mult)
-            if rnd == 2: ts(R("c32", 1, None, 2), R("c32", 1, None, 2), 2 * BL, None, Alu.mult)
-        blocks(AD, "ha", lambda: ts(R("sa", 192, 256), AD, -4096.0, 4094.0, Alu.mult, Alu.add), spare)
+        if rnd == 0: qz(E(3), R("eb", 0, 512))
+        else: fill(R("bw", C, 2 * C), MARK)
+        o = 32 * rnd
+        F, FP, af = R("fi", o, o + 24), R("fp", o, o + 24), R("ha", 0, 24)
+        ts(F, R("csx", 15, None, 16), -1.0 / K, (NZ - 0.5 - B) / K + 0.5, Alu.mult, Alu.add)
+        send(dst, R("fp", o, o + 32), R("fi", o, o + 32), "af%d" % rnd)
+        ts(af, R("csx", 15, None, 16), NZ - B, None, Alu.is_lt)
+        if rnd == 0:
+            for b in (2, 3):
+                mm("pD%d" % b, E(b), QL)
+                minus(b, "pD%d" % b)
+            for b in (0, 1): mm("pD%d" % b, E(b), QX)
+            fill(R("bw", 0, C), MARK)
+        for b in (2, 3): mm(second[b], E(b), QX)
+        for b in range(4): mine(b, second[b] if b > 1 else "pD%d" % b)
+        for b in (2, 3, 0, 1): mm("pD%d" % b, E(b), QX, True, False)
         def diff(b): act(R("zf", b, None, 4), R("pD%d" % b, 0, C), Act.Copy)
-        def theirs(a, b): qz(Q("t", a, b), R("tp", 4 * a, 4 * b))
-        upto(CA, "ha", 0, 0.0)
-        upto(CD, "ha", 1, 0.0)
-        tt(T2, R("sa", 224, 248), TR2, Alu.min)
-        sh, m2 = R("hb", 0, 24), R("hb", 32, 56)
-        tt(R("hb", 0, 64), AD, R("adp", o, o + 64), Alu.min)
-        tt(T1, CA, R("sa", 192, 216), Alu.add)
-        tt(CF, CA, CD, Alu.add)
+        def theirs(i, early):
+            if early == (rnd > 0): qz(Q("t", 128 * i, 128 * i + 128), R("tp", 512 * i, 512 * i + 512))
+        cp(R("ha", 32, 56), F)
+        ts(T2, F, 2.0, 4096.0, Alu.is_lt, Alu.mult)
+        ts(W1, af, -4096.0, 4094.0, Alu.mult, Alu.add)
+        sh, m = R("hb", 0, 24), R("hb", 32, 56)
+        def fill0():
+            tt(T2, T2, TR2, Alu.min)
+            theirs(0, True)
+        def both():
+            theirs(1, True)
+            theirs(2, True)
+            tt(sh, af, FP, Alu.min)
+            tt(m, F, FP, Alu.min)
+        blocks("ha", fill0, both)
         def fill1():
+            upto(CA, "ha", 0, 0.0)
+            upto(CF, "ha", 1, 0.0)
             ts(U1, sh, -4096.0, None, Alu.mult)
-            tt(N2, J2, T1, Alu.min)
-            tt(CF, CF, T2, Alu.add)
-            ts(HB, m2, -4096.0, 4096.0, Alu.mult, Alu.add)
         def fill2():
-            tt(N3, N2, U1, Alu.add)
-            theirs(0, 192)
-        blocks(R("hb", 0, 64), "hb", fill1, fill2)
-        theirs(192, C)
-        for b in range(4): mm("pD%d" % b, E(b), Q("t"), False, True)
-        scan(R("sb", 287, 263, -1), R("hb", 296, 272, -1), R("hb", 359, 335, -1), 1.0, Alu.add, Alu.add)
-        upto(C2, "hb", 1, 0.0)
+            tt(T1, CA, W1, Alu.add)
+            ts(HB, m, 2.0, 4096.0, Alu.is_lt, Alu.mult)
+        if rnd == 0: fill(R("bw", C, 2 * C), MARK)
+        blocks("hb", fill1, fill2)
+        tt(N2, J2, T1, Alu.min)
+        tt(CF, CF, T2, Alu.add)
+        theirs(0, False)
+        behind("sb", 264, "hb", 0, 1.0)
+        tt(N3, N2, U1, Alu.add)
+        upto(CM, "hb", 1, -1.0)
+        behind("sb", 216, "hb", 1, -1.0)
         upto(CS, "hb", 0, -1.0)
-        act(R("sb", 320, 448), R("hb", 272, 400), Act.Copy, accum_out=TOT)
-        act(CT, CF, Act.Identity, bias=TOT)
-        for b in range(4): diff(b)
         tt(POS, N3, SF, Alu.add)
-        tt(CM, CS, C2, Alu.add)
-        tt(POS, POS, CS, Alu.max)
         tt(H, CM, HB, Alu.add)
-        tt(X1, CT, CM, Alu.subtract)
-        cp(oP, POS)
+        tt(X1, CF, SM, Alu.add)
+        theirs(1, False)
+        tt(POS, POS, CS, Alu.max)
         tt(H, H, X1, Alu.min)
-        cp(ind(R("pw"), oP), val)
+        theirs(2, False)
+        for b in (2, 3, 0, 1): mm("pD%d" % b, E(b), Q("t"), False, True)
+        cp(oP, POS)
         ts(oB, H, 2.0, None, Alu.mult)
-        pick(R("ex"), R("pw", 0, NZ), R("c8", 1, 2 * NZ, 2))
+        def seconds(a, b): cp(ind(R("bw"), R("off", 24 + a, 24 + b)), R("nw", NZ + 16 * a, NZ + 16 * b))
+        for b in (2, 3, 0, 1): diff(b)
+        cp(ind(R("pw"), oP), val)
+        seconds(0, S1)
+        for a, b in ((0, K), (K, NZ)): pick(R("ex", a, b), R("pw", a, b), R("c8", 1, 2 * (b - a), 2))
         for a in (0, C):
             if rnd == 0: ts(R("c32", a, a + C, 2), R("tt", 0, 192), qc, float(NZ), Alu.is_equal, Alu.mult)
             if rnd == 1: ts(R("c32", a + 1, a + C, 2), R("tt", 0, 192), qc, 0.5, Alu.is_ge, Alu.subtract)
-        if rnd == 2: ts(R("c32", 31, None, 32), R("c32", 31, None, 32), q17, None, Alu.add)
-        ts(oF(0, NZ), R("ex", 3, None, 4), 4.0, sF, Alu.mult, Alu.add)
+        if rnd == 2:
+            ts(R("c32", 31, None, 32), R("c32", 31, None, 32), q17, None, Alu.add)
+            cp(R("nw", 0, NZ), R("pw", 0, NZ))
+        for a, b in ((0, K), (K, NZ)): ts(oF(a, b), R("ex", a + 3, b, 4), 4.0, sF, Alu.mult, Alu.add)
         T64 = R("w", 4 * NZ)
         act(R("z", 0, 4 * ZA), ind(R("zf"), oF(0, ZA)), Act.Copy)
-        cp(ind(R("bw"), oB), val)
+        seconds(S1, 24)
         cp(R("z", 4 * ZA), ind(R("zf"), oF(ZA, K)))
         act(R("w", 0, 4 * K), ind(T64, oF(0, K)), Act.Copy)
-        act(R("w", 4 * K, 4 * NZ), ind(T64, oF(K, NZ)), Act.Copy)
-        if rnd == 2: act(R("nw", 0, NZ), R("pw", 0, NZ), Act.Copy)
+        act(R("w", 4 * K, 4 * FA), ind(T64, oF(K, FA)), Act.Copy)
         def gsum(b): tt(R("w", b, 4 * K, 4), R(second[b], 0, K), R("w", b, 4 * K, 4), Alu.add)
         ts(R("ur"), R("bw", 0, 2 * C, 2), MARK, None, Alu.is_equal)
         qz(Q("z"), R("z"))
         for b in range(4): mm(second[b], Q("w", 128 * b, 128 * (b + 1)), Q("z"))
         scan(R("bw", 1, 2 * C, 2), R("ones", 0, C), R("ur"), -129.0, Alu.mult, Alu.add)
+        if FA < NZ: cp(R("w", 4 * FA, 4 * NZ), ind(T64, oF(FA, NZ)))
         pick(R("ek", 2 * NZ), R("bw", 2 * NZ, 2 * C), R("c8", 0, 2 * A2))
         pick(R("ek", 0, 2 * NZ), R("bw", 0, 2 * NZ), R("c8", 0, 2 * NZ))
         ts(oN(NZ, C), R("ek", 2 * NZ + 7, None, 8), 4.0, sH, Alu.mult, Alu.add)
@@ -355,33 +395,37 @@ def rank_program(g, core, T, topo):
         for b in range(2, 4): gsum(b)
         def new(a, b): ts(R("xn", 4 * a, 4 * b), ind(R("w"), oN(a, b)), 1.0 / 64, None, Alu.mult)
         act(R("xn", 4 * NZ, 4 * C), ind(R("w", 4 * K), oN(NZ, C)), Act.Copy, scale=1.0 / 64)
-        g1 = G1 if rnd < 2 else G3
-        act(R("xn", 0, 4 * g1), ind(R("w"), oN(0, g1)), Act.Copy, scale=1.0 / 64)
-        if rnd == 2: pick(R("en"), R("bw", 0, 2 * C), R("c32"))
-        new(G2, NZ)
-        if rnd == 2: ts(oL, R("en", 31, None, 32), BL + 128, None, Alu.add)
-        high(rnd + 1)
-        new(g1, G2)
+        def anew(a, b): act(R("xn", 4 * a, 4 * b), ind(R("w"), oN(a, b)), Act.Copy, scale=1.0 / 64)
+        if rnd < 2:
+            anew(0, G1)
+            new(G2, NZ)
+            high(rnd + 1)
+            new(G1, G2)
 
     o = 3 * CP
-    QV = Q("v")
-    mm("pD0", QV, Q("x", o + NZ, o + CP))
-    dma("S", T.oc[:, 4 * NZ:4 * C], raw(R("qx", o + NZ, o + C)))
-    pack(3, 128, NZ)
-    pack(3, 0, 128)
-    act(R("nlb"), ind(R("nw"), oL), Act.Identity, bias=128.0)
-    mm("pD1", QV, Q("x", o + 128, o + NZ))
-    mm("pD2", QV, Q("x", o, o + 128))
+    def codes(a, b, bank):
+        pack(3, a, max(b, a + 128))
+        mm(bank, Q("v"), Q("x", o + a, o + max(b, a + 128)))
+        dma("S", T.oc[:, 4 * a:4 * b], raw(R("qx", o + a, o + b)))
+    pick(R("en"), R("bw", 0, 2 * C), R("c32"))
+    anew(128, L1)
+    anew(0, L2)
+    new(L1, NZ)
+    codes(NZ, C, "pD0")
+    ts(oL, R("en", 31, None, 32), BL + 128, None, Alu.add)
+    new(L2, 128)
+    codes(128, NZ, "pD1")
     cp(R("yb", NZ, C), R("pD0", 0, A2))
-    dma("S", T.oc[:, 0:4 * NZ], raw(R("qx", o, o + NZ)))
+    codes(0, 128, "pD2")
+    act(R("nlb"), ind(R("nw"), oL), Act.Identity, bias=128.0)
     dma("S", T.y[:, NZ:C], R("yb", NZ, C))
+    for k in range(4):
+        add("A", lambda k=k: g.scalar.dma_start(T.osc[4 * k:4 * k + 4, :], T.sx[32 * k:32 * k + 4, o:o + C]), [R("sx", o, o + C)], kind="dma")
     cp(R("yb", 128, NZ), R("pD1", 0, NZ - 128))
     cp(R("yb", 0, 128), R("pD2", 0, 128))
     add("A", lambda: g.scalar.dma_start(T.nl[:], T.nlb[0:128:16, :]), [R("nlb")], kind="dma")
     dma("S", T.y[:, 128:NZ], R("yb", 128, NZ))
-    dma("A", T.y[:, 0:128], R("yb", 0, 128))
-    for k in range(4):
-        add("SA"[k % 2], lambda k=k: queue["SA"[k % 2]].dma_start(T.osc[4 * k:4 * k + 4, :], T.sx[32 * k:32 * k + 4, o:o + C]), [R("sx", o, o + C)], kind="dma")
+    dma("S", T.y[:, 0:128], R("yb", 0, 128))
 
     needed = set()
     for op in ops: needed.update(op["deps"])

import numpy as np
from concourse.mybir import dt, AluOpType, ActivationFunctionType

C, A2, K = 384, 112, 160
NZ = C - A2
CP = NZ + 128
STEP = [1, 2, 3]
BIG = 2.0 ** 90
B = 4096.0
BL = 1792.0
MARK = -512.0
TILES = [["d", 23, 22, 21], [20, 19, 18, 17], [16, 15, 14, 13], [12, 11, 10, 9], [8, 7, 6, 5], [4, 3, 2, 1]]
TN = [384, 320, 256, 192, 128, 128]
VS, VLO, VHI = 1, 15, 21
S1 = 4
FA = 240
ZA = 128
L1, L2 = 200, 72
G1, G2 = 128, 224

F8, U8, BF, F32, F16 = "float8_e4m3fn_x4", "uint8", "bfloat16", "float32", "float16"
SCRATCH = {"ci": ("sbuf", [128, 16], "int32"), "fi": ("sbuf", [128, 96], "int32"), "fp": ("sbuf", [128, 96], "int32"),
           "offu": ("sbuf", [128, 8], "uint16"), "off": ("sbuf", [128, 240], "uint16")}
for _n, _w in [("u", 128), ("u2", 128), ("v", 128), ("w", 512), ("x", 4 * CP), ("xl", 3 * C), ("e", 512), ("g", 128), ("t", C), ("z", K)]:
    SCRATCH["q" + _n] = ("sbuf", [128, _w], F8)
    SCRATCH["s" + _n] = ("sbuf", [128, _w], U8)
for _n, _w in [("x0", 4 * CP), ("xn", 4 * CP), ("ut", 512), ("vt", 512), ("ones", 516), ("eb", 516), ("go", 512),
               ("tt", NZ), ("cm0", 144), ("cmin", 144), ("chold", 144), ("c8", 2 * C), ("c32", 2 * C), ("keep", NZ), ("sig", 8 * 23 * 24), ("ds", C),
               ("ha", 400), ("hb", 400), ("pw", 1440), ("nw", NZ + C), ("bw", 2320), ("ur", C), ("w", 4 * (NZ + C)), ("tp", 4 * C),
               ("zf", 4 * C), ("z", 4 * K), ("jb", 192 * (VHI + 1 - VLO))]:
    SCRATCH[_n] = ("sbuf", [128, _w], BF)
for _n, _w in [("cf", 256), ("cx", C), ("d1", C), ("pb", C), ("jv", C), ("csx", C), ("sa", 256), ("sb", 512), ("nlb", C), ("yb", C)]:
    SCRATCH[_n] = ("sbuf", [128, _w], F32)
for _n, _w in [("ex", NZ), ("ek", 2 * C), ("en", 2 * C)]:
    SCRATCH[_n] = ("sbuf", [128, _w], F16)
for _m in range(6):
    _w = 256 if _m == 3 else TN[_m]
    SCRATCH["bt%d" % _m] = ("sbuf", [128, 4 * TN[_m]], BF)
    SCRATCH["qb%d" % _m] = ("sbuf", [128, _w], F8)
    SCRATCH["sc%d" % _m] = ("sbuf", [128, _w], U8)
for _n in ["pV", "pA", "pC0", "pC1", "pD0", "pD1", "pD2", "pD3"]:
    SCRATCH[_n] = ("psum", [128, 512], F32)
SEMAPHORES = ["cV", "cA", "cP", "cG", "sent"] + ["d%d" % i for i in range(24)] + ["ax%d" % i for i in range(3)] + ["af%d" % i for i in range(3)]


def rank_program(g, core, T, topo):
    rank = T.rank_of(core)
    if rank is None:
        return
    Alu, Act = AluOpType, ActivationFunctionType
    V, S, P = g.vector, g.scalar, g.tensor
    queue = {"V": g.vector, "A": g.scalar, "P": g.tensor, "G": g, "S": g.sync}
    u8, u32 = dt.uint8, dt.uint32
    ops, lastw, lastr, ndma, sent = [], {}, {}, [0], [0]

    def R(n, a=0, b=None, s=1):
        w = SCRATCH[n][1][1]
        if b is None and s > 0: b = w
        return (n, np.arange(w)[a:b:s], T[n][:, a:b:s], [])
    def ind(win, off): return (win[0], win[1], win[2].indirect(off[2]), [off])
    def words(r): return (r[0], r[1], r[2].bitcast(u32), [])
    def raw(r): return (r[0], r[1], r[2].bitcast(u8), [])
    def ap(x): return x[2] if isinstance(x, tuple) else x

    def add(eng, fn, r=(), w=(), kind="c", tok=None, acc=False):
        r = [x for x in r if isinstance(x, tuple)]
        w = [x for x in w if isinstance(x, tuple)]
        r = r + [o for x in r + w for o in x[3]]
        i, deps = len(ops), set()
        who = eng if kind == "c" else i
        for x in r + w:
            if x[0] not in lastw: lastw[x[0]], lastr[x[0]] = np.full(SCRATCH[x[0]][1][1], -1), {}
        def cols(x): return slice(None) if SCRATCH[x[0]][0] == "psum" else x[1]
        for x in r:
            deps.update(np.unique(lastw[x[0]][cols(x)]).tolist())
            if SCRATCH[x[0]][0] == "psum": deps.update(int(a.max()) for e, a in lastr[x[0]].items() if e != who)
        for x in w:
            if not acc: deps.update(np.unique(lastw[x[0]][cols(x)]).tolist())
            deps.update(int(a[cols(x)].max()) for a in lastr[x[0]].values())
        deps.discard(-1)
        if kind == "dma":
            tok = ("d%d" % ndma[0], 16)
            ndma[0] += 1
        ops.append({"eng": eng, "fn": fn, "deps": deps, "kind": kind, "tok": tok})
        if kind != "remote":
            for x in r: lastr[x[0]].setdefault(who, np.full(SCRATCH[x[0]][1][1], -1))[cols(x)] = i
        for x in w: lastw[x[0]][cols(x)] = i

    def ts(o, a, s1, s2, op0, op1=None):
        if op1 is None: add("V", lambda: V.tensor_scalar(o[2], a[2], ap(s1), None, op0), [a, s1], [o])
        else: add("V", lambda: V.tensor_scalar(o[2], a[2], ap(s1), ap(s2), op0, op1), [a, s1, s2], [o])
    def tt(o, a, b, op): add("V", lambda: V.tensor_tensor(o[2], a[2], b[2], op), [a, b], [o])
    def scan(o, a, b, init, op0, op1): add("V", lambda: V.tensor_tensor_scan(o[2], a[2], b[2], init, op0, op1), [a, b], [o])
    def pick(o, a, c): scan(o, a, c, -2 * B, Alu.max, Alu.add)
    def cp(o, a): add("V", lambda: V.tensor_copy(o[2], a[2]), [a], [o])
    def tr(o, a): add("V", lambda: V.transpose(o[2], a[2]), [a], [o])
    def fill(o, c): add("V", lambda: V.memset(o[2], c), [], [o])
    def act(o, a, f, **kw): add("A", lambda: S.activation(o[2], a[2], f, **{k: ap(x) for k, x in kw.items()}), [a, kw.get("bias"), kw.get("scale")], [o, kw.get("accum_out")])
    def Q(n, a=0, b=None): return (R("q" + n, a, b), R("s" + n, a, b))
    def qz(q, a): add("V", lambda: V.quantize_mx(q[0][2], q[1][2], a[2]), [a], q)
    def mm(bank, l, x, st=True, sp=True):
        o = R(bank, 0, len(x[0][1]))
        add("P", lambda: P.matmul_mx(o[2], l[0][2], l[1][2], x[0][2], x[1][2], st, sp), l + x, [o], acc=not st)
    def dma(e, o, a): add(e, lambda: queue[e].dma_start(ap(o), ap(a)), [a], [o], kind="dma")
    def send(dst, o, a, sem):
        rid, pid, _ = topo.addr(dst)
        sent[0] += len(topo.engines(core, dst))
        add("G", lambda: g.remote_dma(o[2], a[2], T.sem[sem], T.sem.sent, pid, rid, topo.mask(core, dst)), [a], kind="remote")
    def iota(o, pat, base, cm):
        kw = {} if o[0] in ("ci", "fi") else {"allow_small_or_imprecise_dtypes": True}
        add("G", lambda: g.iota(o[2], pat, base, cm, **kw), [], [o])

    dma("S", R("ut", 0, 256), T.u[:, 0:256])
    dma("A", R("ut", 256), T.u[:, 256:512])
    dma("S", R("x0", 4 * NZ, 4 * C), T.x[:, 4 * NZ:4 * C])
    dma("A", R("x0", 0, 512), T.x[:, 0:512])
    dma("S", R("x0", 512, 4 * NZ), T.x[:, 512:4 * NZ])
    qc, gq, qa, qr, qd, ng, r4, b4, e4, sF, sN, sH, q17 = [R("cf", i, i + 1) for i in (0, 1, 4, 5, 6, 7, 2, 3, 8, 9, 10, 11, 12)]
    K16, J, KA, J2, TR2 = [R("cf", 16 + 24 * i, 40 + 24 * i) for i in range(5)]
    val = R("nw", NZ)
    ci = lambda a, b: R("ci", a, b)
    iota(ci(0, 1), [[0, 1]], 0, 1)
    fill(R("ones"), 1.0)
    iota(K16, [[16, 24]], 0, 0)
    iota(R("tt"), [[0, 17], [1, 16]], 0, 0)
    add("G", lambda: g.affine_select(T.eb[:], T.ones[:], [[-1, 516]], Alu.is_equal, 0.0, 3, 4), [R("ones")], [R("eb")])
    ts(ci(1, 2), ci(0, 1), 15, None, Alu.bitwise_and)
    ts(ci(2, 3), ci(0, 1), 0x70, None, Alu.bitwise_and)
    ts(ci(3, 4), ci(0, 1), 2, 3, Alu.arith_shift_right, Alu.bitwise_and)
    ts(ci(4, 5), ci(0, 1), 3, None, Alu.bitwise_and)
    tail = lambda m: fill(R("bt%d" % m, 64 * TILES[m][3] if m < 5 else 0), 0.0)
    fill(R("x0", 4 * C), 0.0)
    cp(R("offu"), R("cf", 16, 24))
    for m in (0, 1): tail(m)
    cp(R("cf", 0, 4), ci(1, 5))
    tail(5)
    ts(R("cf", 200, 208), R("cf", 16, 24), gq, None, Alu.is_equal)
    ts(qa, qc, -0.5, None, Alu.add)
    ts(R("cm0"), R("tt", 0, 144), qc, 0.5, Alu.is_equal, Alu.subtract)
    qz(Q("u"), R("ut"))
    ts(R("chold"), R("tt", 0, 144), qa, -2 * BIG, Alu.subtract, Alu.mult)
    qz((R("qb3", 128), R("sc3", 128)), R("bt5"))
    act(qr, qc, Act.Identity, scale=-2 * B, bias=B)
    act(ng, qc, Act.Identity, scale=-2 * B, bias=30 * B)
    act(qd, qc, Act.Square, bias=-16.0)
    act(J, K16, Act.Identity, bias=qc)
    act(R("keep"), R("tt"), Act.Sign)
    act(R("cmin"), R("cm0"), Act.Copy, scale=2 * BIG)
    act(R("su2"), ind(R("su"), R("offu")), Act.Copy)
    for j in range(8): act(R("go", 64 * j, 64 * j + 64), R("ones", 0, 64), Act.Copy, scale=R("cf", 200 + j, 201 + j))
    E = lambda b: Q("e", 128 * b, 128 * (b + 1))
    cp(words(R("qu2")), ind(words(R("qu")), R("offu")))
    for a, b in ((NZ, CP), (0, 128), (128, NZ)): qz(Q("x", a, b), R("x0", 4 * a, 4 * b))
    for bank in ("pD0", "pD1"): mm(bank, Q("u2"), Q("x", NZ, CP))
    for m in (2, 3, 4): tail(m)
    act(qd, qd, Act.Identity, scale=-B, bias=ng)
    for a in (0, 192): act(R("cx", a, a + 192), R("tt", 0, 192), Act.Identity, scale=2 * B, bias=qr)
    act(KA, J, Act.Identity, bias=qd)
    act(sH, r4, Act.Identity, scale=-2 * BL, bias=BL)
    act(e4, r4, Act.Square, bias=-4.0)
    act(sF, b4, Act.Identity, bias=4 * (BL + 128))
    act(R("cf", 64 + VLO, 65 + VHI), R("cf", 64 + VLO, 65 + VHI), Act.Identity, bias=-128.0)
    def lists():
        act(R("cf", 208, 212), R("tt", 0, 4), Act.Identity, scale=2 * BL, bias=sH)
        act(e4, e4, Act.Identity, scale=-BL, bias=-BL)
        act(sN, r4, Act.Identity, scale=4.0 * NZ, bias=sF)
        act(J2, J, Act.Identity, bias=float(NZ), scale=2.0)
        act(TR2, J, Act.Identity, bias=float(C + 1))
        act(R("cf", 211, 212), R("cf", 211, 212), Act.Identity, bias=e4)
        act(sN, sN, Act.Identity, bias=-12.0 * NZ)
        for t in range(4): act(R("c8", 2 * t + 1, None, 8), R("ones", 0, 96), Act.Copy, scale=R("cf", 208 + t, 209 + t))
        act(sH, sN, Act.Identity, bias=-4.0 * K)
        act(R("c8", 0, None, 2), R("ones", 0, C), Act.Copy, scale=float(NZ))
    U2 = Q("u2")

    place = {}
    for m in range(6):
        for t in range(4): place[TILES[m][t]] = (m, t)
    def plane(k, a, b):
        m, t = place[k]
        return R("bt%d" % m, 4 * a + t, 4 * b, 4)
    piv = lambda k: R("pb", 16 * k, 16 * k + 1)
    second = ["pV", "pA", "pC1", "pC0"]
    def relu(k): act(plane(k, 0, 16 * k), R("sig", 8 * k * (k - 1), 8 * k * (k + 1)), Act.Relu, accum_out=R("jv", 16 * k + 15, 16 * k + 16))
    def sign(k, a, b, src): act(R("sig", 8 * k * (k - 1) + a, 8 * k * (k - 1) + b), src, Act.Sign, bias=piv(k), scale=-1.0)
    def back(n, lo, hi): return R(n, hi - 1, lo - 1 if lo else None, -1)
    def own(lo, hi, src): tt(R("d1", lo, hi), src, R("cmin", 0, hi - lo), Alu.min)
    def hold(lo, hi): scan(back("pb", lo, hi), back("chold", 0, hi - lo), back("d1", lo, hi), 0.0, Alu.min, Alu.max)

    def blocks(h, fill1, fill2):
        tr(R(h, 64, 128), R(h, 0, 64))
        fill1()
        scan(R(h, 144, 208), R("keep", 0, 64), R(h, 64, 128), 0.0, Alu.mult, Alu.add)
        scan(R(h, 271, 207, -1), R(h, 128, 64, -1), R("keep", 0, 64), 0.0, Alu.add, Alu.mult)
        fill2()
        tr(R(h, 272, 400), R(h, 144, 272))
    def upto(out, h, i, init): scan(out, R(h, 335 + 32 * i, 359 + 32 * i), R(h, 272 + 32 * i, 296 + 32 * i), init, Alu.add, Alu.add)
    def behind(n, a, h, i, init): scan(back(n, a, a + 24), back(h, 273 + 32 * i, 297 + 32 * i), back(h, 336 + 32 * i, 360 + 32 * i), init, Alu.add, Alu.add)

    KD, W1, T2, CA, N2, CF, T1 = [R("sa", 24 * i, 24 * (i + 1)) for i in range(7)]
    U1, N3, CS, POS, CM, X1, HB, H = [R("sb", 24 * i, 24 * (i + 1)) for i in range(8)]
    SM, SF = R("sb", 216, 240), R("sb", 264, 288)
    oP, oB, oL = R("off", 0, 24), R("off", 24, 48), R("off", 48, 72)
    oF = lambda a, b: R("off", 72 + a // 4, 72 + b // 4)
    oN = lambda a, b: R("off", 140 + a // 4, 140 + b // 4)
    state = lambda rnd: "x0" if rnd == 0 else "xn"
    def pack(rnd, a, b): qz(Q("x", CP * rnd + a, CP * rnd + b), R(state(rnd), 4 * a, 4 * b))
    def high(rnd):
        pack(rnd, NZ, CP)
        if rnd < 3:
            for bank in ("pD0", "pD1"): mm(bank, U2, Q("x", CP * rnd + NZ, CP * (rnd + 1)))

    for rnd in range(3):
        QX, QL = Q("x", CP * rnd, CP * rnd + C), Q("xl", C * rnd, C * (rnd + 1))
        dst = T.cores[rank ^ STEP[rnd]]
        ne = len(topo.engines(dst, core))
        own(NZ, C, R("pD0", 0, A2))
        if rnd == 0:
            qz(Q("g"), R("go"))
            qz(E(1), R("eb", 2, 514))
        else:
            pack(rnd, 0, 128)
            pack(rnd, 128, NZ)
        hold(NZ, C)
        if rnd == 0: qz(E(0), R("eb", 3, 515))
        if rnd == 1:
            qz(Q("v"), R("vt"))
            ts(q17, qc, -17.0, BL, Alu.add, Alu.mult)
        if rnd == 2: ts(R("c32", 1, None, 2), R("c32", 1, None, 2), 2 * BL, None, Alu.mult)
        for bank in ("pA", "pV"): mm(bank, U2, Q("x", CP * rnd, CP * rnd + NZ))
        def compare(k, a, b, src): ts(plane(k, a, b), src, piv(k), None, Alu.is_lt)
        def within(a, b, src): tt(plane("d", a, b), src, R("pb", a, b), Alu.is_lt)
        def inblock(a, b): scan(R("ds", a, b), R("keep", 0, b - a), plane("d", a, b), 0.0, Alu.mult, Alu.add)
        within(NZ, C, R("pD0", 0, A2))
        for k in range(VHI, 17, -1): compare(k, NZ, 16 * k, R("pD0", 0, 16 * k - NZ))
        inblock(NZ, C)
        for k in range(23, VHI, -1): sign(k, NZ, 16 * k, R("pD1", 0, 16 * k - NZ))
        send(dst, raw(QL[0]), raw(QX[0]), "ax%d" % rnd)
        send(dst, QL[1], QX[1], "ax%d" % rnd)
        add("-", None, w=QL, kind="ext", tok=("ax%d" % rnd, 2 * ne))
        add("-", None, w=[R("fp", 32 * rnd, 32 * rnd + 32)], kind="ext", tok=("af%d" % rnd, ne))
        if rnd == 0:
            for z in (R("jv", 15, 16), R("fi"), R("ha", 0, 144), R("hb", 0, 144), R("xn", 4 * C)): iota(z, [[0, len(z[1])]], 0, 0)
            iota(val, [[1, C]], -128, 0)
            add("S", lambda: g.sync.dma_start(T.qw[:].bitcast(u8), T.wc[:]), QL, [R("qw")], kind="dma")
            dma("S", R("vt"), T.v[:])
            dma("S", R("sw"), T.ws[:])
        G = Q("g")
        def tile(m):
            q = lambda a, b: (R("qb%d" % m, a, b), R("sc%d" % m, a, b))
            qz(q(0, TN[m]), R("bt%d" % m, 0, 4 * TN[m]))
            mm("pC0", G, q(0, 128), m == 0, m == 5)
            if m < 4: mm("pC1", G, q(128, max(256, TN[m])), m == 0, m == 3)
        def low(k): compare(k, 0, min(16 * k, NZ), R("pV", 0, min(16 * k, NZ)))
        def lowsign(k): sign(k, 0, min(16 * k, NZ), R("pA", 0, min(16 * k, NZ)))
        def rows(k):
            e = 192 * (k - VLO + 1)
            scan(R("jb", e - 8 * k, e), plane(k, 0, 8 * k), plane(k, 8 * k, 16 * k), -128.0, Alu.add, Alu.add)
        if rnd > 0:
            for b in (0, 1): mm("pD%d" % b, E(b), QX)
        own(128, NZ, R("pV", 128, NZ))
        own(0, 128, R("pV", 0, 128))
        low(VHI)
        hold(128, NZ)
        hold(0, 128)
        for k in range(23, VHI, -1): lowsign(k)
        for k in range(23, VHI, -1): relu(k)
        ks = list(range(VLO - 1, VS, -1))
        for i in range(len(ks) + 4):
            if i < len(ks): lowsign(ks[i])
            if i >= 4: relu(ks[i - 4])
        low(VHI - 1)
        within(0, NZ, R("pV", 0, NZ))
        for k in range(VHI - 2, 16, -1): low(k)
        tile(0)
        for k in range(16, VLO - 1, -1): low(k)
        tile(1)
        inblock(0, NZ)
        tile(2)
        if rnd > 0:
            for b in (2, 3): mm("pD%d" % b, E(b), QL)
        for k in range(VHI, VHI - 3, -1): rows(k)
        for k in range(1, VS + 1): low(k)
        tile(3)
        tt(KD, KA, R("ds", 15, None, 16), Alu.subtract)
        for k in range(VHI - 3, VLO - 1, -1): rows(k)
        for k in range(1, VS + 1): scan(R("jv", 16 * k + 16 - 8 * k, 16 * k + 16), plane(k, 0, 8 * k), plane(k, 8 * k, 16 * k), 0.0, Alu.add, Alu.add)
        def less(a, b, sums): tt(R("cx", 16 * a + 15, 16 * b, 16), R("sa", a, b), sums, Alu.subtract)
        less(VHI + 1, 24, R("jv", 16 * VHI + 31, C, 16))
        tile(4)
        less(8, VLO, R("jv", 143, 16 * VLO, 16))
        less(VLO, VHI + 1, R("jb", 191, None, 192))
        tile(5)
        def mine(b, bank): act(R("w", 4 * NZ + b, None, 4), R(bank, 0, C), Act.Copy, scale=64.0)
        def minus(b, bank): act(R("tp", b, None, 4), R(bank, 0, C), Act.Copy, scale=-1.0)
        if rnd == 0: lists()
        else:
            for b in (2, 3): minus(b, "pD%d" % b)
        for b, bank in ((0, "pA"), (1, "pV")):
            mm(bank, E(b), QL)
            minus(b, bank)
        less(0, 8, R("jv", 15, 128, 16))
        pick(R("csx", 128, C), R("pC1", 0, 256), R("cx", 128, C))
        if rnd == 0: qz(E(2), R("eb", 1, 513))
        else: fill(R("bw", 0, C), MARK)
        pick(R("csx", 0, 128), R("pC0", 0, 128), R("cx", 0, 128))
        if rnd == 0: qz(E(3), R("eb", 0, 512))
        else: fill(R("bw", C, 2 * C), MARK)
        o = 32 * rnd
        F, FP, af = R("fi", o, o + 24), R("fp", o, o + 24), R("ha", 0, 24)
        ts(F, R("csx", 15, None, 16), -1.0 / K, (NZ - 0.5 - B) / K + 0.5, Alu.mult, Alu.add)
        send(dst, R("fp", o, o + 32), R("fi", o, o + 32), "af%d" % rnd)
        ts(af, R("csx", 15, None, 16), NZ - B, None, Alu.is_lt)
        if rnd == 0:
            for b in (2, 3):
                mm("pD%d" % b, E(b), QL)
                minus(b, "pD%d" % b)
            for b in (0, 1): mm("pD%d" % b, E(b), QX)
            fill(R("bw", 0, C), MARK)
        for b in (2, 3): mm(second[b], E(b), QX)
        for b in range(4): mine(b, second[b] if b > 1 else "pD%d" % b)
        for b in (2, 3, 0, 1): mm("pD%d" % b, E(b), QX, True, False)
        def diff(b): act(R("zf", b, None, 4), R("pD%d" % b, 0, C), Act.Copy)
        def theirs(i, early):
            if early == (rnd > 0): qz(Q("t", 128 * i, 128 * i + 128), R("tp", 512 * i, 512 * i + 512))
        cp(R("ha", 32, 56), F)
        ts(T2, F, 2.0, 4096.0, Alu.is_lt, Alu.mult)
        ts(W1, af, -4096.0, 4094.0, Alu.mult, Alu.add)
        sh, m = R("hb", 0, 24), R("hb", 32, 56)
        def fill0():
            tt(T2, T2, TR2, Alu.min)
            theirs(0, True)
        def both():
            theirs(1, True)
            theirs(2, True)
            tt(sh, af, FP, Alu.min)
            tt(m, F, FP, Alu.min)
        blocks("ha", fill0, both)
        def fill1():
            upto(CA, "ha", 0, 0.0)
            upto(CF, "ha", 1, 0.0)
            ts(U1, sh, -4096.0, None, Alu.mult)
        def fill2():
            tt(T1, CA, W1, Alu.add)
            ts(HB, m, 2.0, 4096.0, Alu.is_lt, Alu.mult)
        if rnd == 0: fill(R("bw", C, 2 * C), MARK)
        blocks("hb", fill1, fill2)
        tt(N2, J2, T1, Alu.min)
        tt(CF, CF, T2, Alu.add)
        theirs(0, False)
        behind("sb", 264, "hb", 0, 1.0)
        tt(N3, N2, U1, Alu.add)
        upto(CM, "hb", 1, -1.0)
        behind("sb", 216, "hb", 1, -1.0)
        upto(CS, "hb", 0, -1.0)
        tt(POS, N3, SF, Alu.add)
        tt(H, CM, HB, Alu.add)
        tt(X1, CF, SM, Alu.add)
        theirs(1, False)
        tt(POS, POS, CS, Alu.max)
        tt(H, H, X1, Alu.min)
        theirs(2, False)
        for b in (2, 3, 0, 1): mm("pD%d" % b, E(b), Q("t"), False, True)
        cp(oP, POS)
        ts(oB, H, 2.0, None, Alu.mult)
        def seconds(a, b): cp(ind(R("bw"), R("off", 24 + a, 24 + b)), R("nw", NZ + 16 * a, NZ + 16 * b))
        for b in (2, 3, 0, 1): diff(b)
        cp(ind(R("pw"), oP), val)
        seconds(0, S1)
        for a, b in ((0, K), (K, NZ)): pick(R("ex", a, b), R("pw", a, b), R("c8", 1, 2 * (b - a), 2))
        for a in (0, C):
            if rnd == 0: ts(R("c32", a, a + C, 2), R("tt", 0, 192), qc, float(NZ), Alu.is_equal, Alu.mult)
            if rnd == 1: ts(R("c32", a + 1, a + C, 2), R("tt", 0, 192), qc, 0.5, Alu.is_ge, Alu.subtract)
        if rnd == 2:
            ts(R("c32", 31, None, 32), R("c32", 31, None, 32), q17, None, Alu.add)
            cp(R("nw", 0, NZ), R("pw", 0, NZ))
        for a, b in ((0, K), (K, NZ)): ts(oF(a, b), R("ex", a + 3, b, 4), 4.0, sF, Alu.mult, Alu.add)
        T64 = R("w", 4 * NZ)
        act(R("z", 0, 4 * ZA), ind(R("zf"), oF(0, ZA)), Act.Copy)
        seconds(S1, 24)
        cp(R("z", 4 * ZA), ind(R("zf"), oF(ZA, K)))
        act(R("w", 0, 4 * K), ind(T64, oF(0, K)), Act.Copy)
        act(R("w", 4 * K, 4 * FA), ind(T64, oF(K, FA)), Act.Copy)
        def gsum(b): tt(R("w", b, 4 * K, 4), R(second[b], 0, K), R("w", b, 4 * K, 4), Alu.add)
        ts(R("ur"), R("bw", 0, 2 * C, 2), MARK, None, Alu.is_equal)
        qz(Q("z"), R("z"))
        for b in range(4): mm(second[b], Q("w", 128 * b, 128 * (b + 1)), Q("z"))
        scan(R("bw", 1, 2 * C, 2), R("ones", 0, C), R("ur"), -129.0, Alu.mult, Alu.add)
        if FA < NZ: cp(R("w", 4 * FA, 4 * NZ), ind(T64, oF(FA, NZ)))
        pick(R("ek", 2 * NZ), R("bw", 2 * NZ, 2 * C), R("c8", 0, 2 * A2))
        pick(R("ek", 0, 2 * NZ), R("bw", 0, 2 * NZ), R("c8", 0, 2 * NZ))
        ts(oN(NZ, C), R("ek", 2 * NZ + 7, None, 8), 4.0, sH, Alu.mult, Alu.add)
        for b in range(2): gsum(b)
        ts(oN(0, NZ), R("ek", 7, 2 * NZ, 8), 4.0, sN, Alu.mult, Alu.add)
        for b in range(2, 4): gsum(b)
        def new(a, b): ts(R("xn", 4 * a, 4 * b), ind(R("w"), oN(a, b)), 1.0 / 64, None, Alu.mult)
        act(R("xn", 4 * NZ, 4 * C), ind(R("w", 4 * K), oN(NZ, C)), Act.Copy, scale=1.0 / 64)
        def anew(a, b): act(R("xn", 4 * a, 4 * b), ind(R("w"), oN(a, b)), Act.Copy, scale=1.0 / 64)
        if rnd < 2:
            anew(0, G1)
            new(G2, NZ)
            high(rnd + 1)
            new(G1, G2)

    o = 3 * CP
    def codes(a, b, bank):
        pack(3, a, max(b, a + 128))
        mm(bank, Q("v"), Q("x", o + a, o + max(b, a + 128)))
        dma("S", T.oc[:, 4 * a:4 * b], raw(R("qx", o + a, o + b)))
    pick(R("en"), R("bw", 0, 2 * C), R("c32"))
    anew(128, L1)
    anew(0, L2)
    new(L1, NZ)
    codes(NZ, C, "pD0")
    ts(oL, R("en", 31, None, 32), BL + 128, None, Alu.add)
    new(L2, 128)
    codes(128, NZ, "pD1")
    cp(R("yb", NZ, C), R("pD0", 0, A2))
    codes(0, 128, "pD2")
    act(R("nlb"), ind(R("nw"), oL), Act.Identity, bias=128.0)
    dma("S", T.y[:, NZ:C], R("yb", NZ, C))
    for k in range(4):
        add("A", lambda k=k: g.scalar.dma_start(T.osc[4 * k:4 * k + 4, :], T.sx[32 * k:32 * k + 4, o:o + C]), [R("sx", o, o + C)], kind="dma")
    cp(R("yb", 128, NZ), R("pD1", 0, NZ - 128))
    cp(R("yb", 0, 128), R("pD2", 0, 128))
    add("A", lambda: g.scalar.dma_start(T.nl[:], T.nlb[0:128:16, :]), [R("nlb")], kind="dma")
    dma("S", T.y[:, 128:NZ], R("yb", 128, NZ))
    dma("S", T.y[:, 0:128], R("yb", 0, 128))

    needed = set()
    for op in ops: needed.update(op["deps"])
    count = {"V": 0, "A": 0, "P": 0, "G": 0}
    for i, op in enumerate(ops):
        if op["kind"] == "c" and i in needed:
            count[op["eng"]] += 1
            op["tok"] = ("c" + op["eng"], count[op["eng"]])
    waited = {e: {} for e in queue}
    seen = {}
    for op in ops:
        if op["kind"] == "ext": continue
        e = op["eng"]
        want = {}
        for d in op["deps"]:
            s, v = ops[d]["tok"]
            want[s] = max(want.get(s, 0), v)
        for s in sorted(want):
            if waited[e].get(s, 0) < want[s]:
                queue[e].wait_ge(T.sem[s], want[s])
                waited[e][s] = want[s]
                seen[s] = max(seen.get(s, 0), want[s])
        ins = op["fn"]()
        if op["kind"] == "dma": ins.then_inc(T.sem[op["tok"][0]], 16)
        elif op["kind"] == "c" and op["tok"]: ins.then_inc(T.sem[op["tok"][0]], 1)
    g.wait_ge(T.sem.sent, sent[0])
    for i in range(ndma[0]):
        if seen.get("d%d" % i, 0) < 16: g.sync.wait_ge(T.sem["d%d" % i], 16)
